import numpy as np
import ml_dtypes


def mxq(x, axis, fmt="e4m3"):
    dtype, down = {"e4m3": (ml_dtypes.float8_e4m3fn, 7), "e5m2": (ml_dtypes.float8_e5m2, 14)}[fmt]
    v = np.moveaxis(np.asarray(x, np.float32).astype(ml_dtypes.bfloat16).astype(np.float64), axis, -1)
    blocks = v.reshape(v.shape[:-1] + (-1, 32))
    amax = np.abs(blocks).max(-1, keepdims=True)
    byte = np.maximum(np.where(amax > 0, np.frexp(amax)[1] - 1 + 127, 0) - down, 1)
    scale = np.exp2(byte - 127.0)
    codes = (blocks / scale).astype(np.float32).astype(dtype).astype(np.float64)
    return np.moveaxis((codes * scale).reshape(v.shape), -1, axis)


WIDE = False


def mx_kscale(k):
    if not WIDE:
        return np.ones(k)
    levels = np.array([10, -10, 5, -5, 0])
    if k % 512:
        return np.exp2(np.random.permutation(np.resize(levels, k // 32))).repeat(32)
    a = np.empty((k // 512, 16))
    for p in range(k // 512):
        a[p, :8] = np.random.permutation(np.resize(levels, 8))
        for g in range(8):
            far = levels[np.abs(levels - a[p, g]) >= 10]
            a[p, g + 8] = far[np.random.randint(len(far))]
    return np.exp2(a.ravel()).repeat(32)


def f64(x):
    return np.asarray(x).astype(np.float64)


def striped(idx):
    return np.tile(idx.reshape(-1, 16).T, (8, 1)).astype(np.uint16)


def unstriped(offs):
    return offs[:16].T.reshape(-1).astype(np.int64)


def striped8(idx):
    return np.concatenate([x.reshape(-1, 16).T for x in idx]).astype(np.uint16)


def runs(offs, k):
    lists = np.stack([offs[16 * r : 16 * r + 16].T.reshape(-1) for r in range(8)]).astype(np.int64)
    return lists[np.arange(k) % 512 // 64]


def pack_weight(w):
    k, n = w.shape
    w = f64(np.asarray(w, np.float32).astype(ml_dtypes.bfloat16)).reshape(k // 32, 32, n)
    amax = np.abs(w).max(1)
    byte = np.clip(np.where(amax > 0, np.frexp(amax)[1] - 1 + 127 - 7, 1), 1, 254)
    scaled = (w * np.exp2(127.0 - byte)[:, None, :]).reshape(k, n).astype(np.float32)
    words = np.ascontiguousarray(scaled.reshape(k // 512, 128, 4, n).transpose(0, 1, 3, 2)).astype(ml_dtypes.float8_e4m3fn).view(np.uint8)
    return words, np.ascontiguousarray(byte.astype(np.uint8).reshape(k // 512, 16, n))


def unpack_weight(words, scales):
    g, p, n, _ = words.shape
    vals = np.ascontiguousarray(words).view(ml_dtypes.float8_e4m3fn).astype(np.float64) * np.repeat(np.exp2(scales.astype(np.float64) - 127.0), 8, axis=1)[..., None]
    return vals.transpose(0, 1, 3, 2).reshape(g * 512, n)


def relu(v):
    return np.maximum(v, 0.0)

def planes(y):
    n, m = y.shape
    v = y.astype(np.float32).astype(ml_dtypes.bfloat16).astype(np.float64).reshape(n // 32, 32, m)
    top = np.abs(v).max(1)
    byte = np.clip(np.where(top > 0, np.frexp(top)[1] - 1 + 127 - 7, 1), 1, 254)
    codes = (v * np.exp2(127.0 - byte)[:, None, :]).reshape(n, m).astype(np.float32).astype(ml_dtypes.float8_e4m3fn).view(np.uint8)
    words = codes.reshape(n // 512, 128, 4, m).transpose(0, 1, 3, 2)
    return np.ascontiguousarray(words), np.ascontiguousarray(byte.astype(np.uint8).reshape(n // 512, 16, m))


K, T, S, N, H = 512, 2048, 512, 512, 512


def setup_inputs():
    n = np.random.standard_normal
    s = mx_kscale(K)[:, None]
    u = mx_kscale(H)
    packed_xT = pack_weight(n((K, T)) * s)
    packed_w1 = pack_weight(n((K, H)) / np.sqrt(K) / s)
    packed_w2 = pack_weight(n((H, N)) / np.sqrt(H) / u[:, None])
    return {
        "x_words": packed_xT[0],
        "x_scales": packed_xT[1],
        "w1_words": packed_w1[0],
        "w1_scales": packed_w1[1],
        "gn": (np.random.uniform(0.5, 1.5, (H, 1)) * u[:, None]).astype(np.float32),
        "w2_words": packed_w2[0],
        "w2_scales": packed_w2[1],
        "offs": striped(np.random.permutation(T)[:S]),
        "east": striped8(np.stack([np.random.permutation(S) for _ in range(8)])),
        "west": striped8(np.stack([np.random.permutation(S) for _ in range(8)])),
    }


def reference(x_words, x_scales, w1_words, w1_scales, gn, w2_words, w2_scales, offs, east, west):
    xq = unpack_weight(x_words, x_scales)[:, unstriped(offs)]
    y = unpack_weight(w1_words, w1_scales).T @ xq
    a = y - (y[np.arange(H)[:, None], runs(west, H)])
    b = y[np.arange(H)[:, None], runs(east, H)] - y
    mn = np.minimum(a, b)
    mx = np.maximum(a, b)
    z = f64(gn) * (y + 0.5 * (relu(mn) + mx - relu(mx)))
    out_0 = unpack_weight(w2_words, w2_scales).T @ mxq(z, 0, "e4m3")
    return (out_0,) + planes(out_0)

@@ -1,0 +1,232 @@
+from contextlib import ExitStack
+
+import concourse.mybir as mybir
+
+K, T, S, N, H = 512, 2048, 512, 512, 512
+FLOPS = 2 * K * H * S + 2 * H * N * S
+
+F32 = mybir.dt.float32
+BF16 = mybir.dt.bfloat16
+I32 = mybir.dt.int32
+U32 = mybir.dt.uint32
+U16 = mybir.dt.uint16
+U8 = mybir.dt.uint8
+FP8X4 = mybir.dt.float8_e4m3fn_x4
+ALU = mybir.AluOpType
+COPY = mybir.ActivationFunctionType.Copy
+
+P = 128
+PACK = 4
+HALF = S // 2
+PIECE = 128
+
+
+def tile_picked_minmod_none_po_kernel(
+    tc, x_words, x_scales, w1_words, w1_scales, gn, w2_words, w2_scales, offs, east, west, out_0, out_1, out_2
+):
+    nc = tc.nc
+    with ExitStack() as ctx:
+        keep = ctx.enter_context(tc.tile_pool(name="keep", bufs=1))
+        psum = ctx.enter_context(tc.psum_pool(name="psum", bufs=8))
+
+        def sb(name, shape, dtype):
+            return keep.tile(shape, dtype, name=name, align_bytes=64)
+
+        def bank(name, shape):
+            return psum.tile(shape, F32, name=name, tag="bank")
+
+        def words_of(dram):
+            return dram[0].rearrange("p n t -> p (n t)").bitcast(I32)
+
+        def load_scale_rows(queue, tile, dram, q):
+            queue.dma_start(out=tile[32 * q : 32 * q + 4, :].bitcast(I32), in_=dram[0, 4 * q : 4 * q + 4, :].bitcast(I32))
+
+        offs_sb = keep.tile([P, S // 16], U16, name="offs_sb")
+        east_sb = keep.tile([P, S // 16], U16, name="east_sb")
+        west_sb = keep.tile([P, S // 16], U16, name="west_sb")
+        xw = sb("xw", [P, T], U32)
+        xs = sb("xs", [P, T], U8)
+        w1w = sb("w1w", [P, H], I32)
+        w1s = sb("w1s", [P, H], U8)
+        w2w = sb("w2w", [P, N], I32)
+        w2s = sb("w2s", [P, N], U8)
+        gain = sb("gain", [P, PACK], F32)
+
+        for plane in (xs, w1s, w2s):
+            nc.vector.memset(plane[:].bitcast(I32), 0)
+
+        nc.gpsimd.dma_start(out=gain[:], in_=gn.rearrange("(p t) o -> p (t o)", t=PACK))
+        nc.sync.dma_start(offs_sb[:], offs)
+        nc.sync.dma_start(east_sb[:], east)
+        nc.sync.dma_start(out=xw[:].bitcast(I32), in_=words_of(x_words))
+        for q in range(4):
+            load_scale_rows(nc.sync, xs, x_scales, q)
+        nc.sync.dma_start(out=w1w[:], in_=words_of(w1_words))
+        for q in range(4):
+            load_scale_rows(nc.sync if q < 2 else nc.gpsimd, w1s, w1_scales, q)
+        nc.sync.dma_start(out=w2w[:], in_=words_of(w2_words))
+        nc.sync.dma_start(west_sb[:], west)
+        for q in range(4):
+            load_scale_rows(nc.sync, w2s, w2_scales, q)
+
+        half_gain = sb("half_gain", [P, PACK], F32)
+        minus_half_gain = sb("minus_half_gain", [P, PACK], F32)
+        nc.scalar.activation(half_gain[:], gain[:], COPY, scale=0.5)
+        nc.scalar.activation(minus_half_gain[:], gain[:], COPY, scale=-0.5)
+
+        def deal(name, words, scales):
+            dealt_words = sb(name + "_words", [P, 512], I32)
+            dealt_scales = sb(name + "_scales", [P, 512], U8)
+            nc.vector.tensor_copy(
+                out=dealt_words[:].rearrange("p (t b i) -> p b t i", t=PACK, i=4),
+                in_=words[:].rearrange("p (b i t) -> p b t i", t=PACK, i=4),
+            )
+            nc.vector.tensor_copy(
+                out=dealt_scales[:].rearrange("p (t b i) -> p b t i", t=PACK, i=16),
+                in_=scales[:].rearrange("p (b i t) -> p b t i", t=PACK, i=16),
+            )
+            return dealt_words, dealt_scales
+
+        picked_scales = sb("picked_scales", [P, S], U8)
+        picked_words = sb("picked_words", [P, S], U32)
+        nc.vector.tensor_copy(picked_scales[:], xs[:].indirect(offs_sb[:]))
+        halves = [slice(0, HALF), slice(HALF, S)]
+        list_halves = [slice(0, HALF // 16), slice(HALF // 16, S // 16)]
+        nc.vector.tensor_copy(picked_words[:, halves[0]], xw[:].indirect(offs_sb[:, list_halves[0]]))
+        w1_dealt = deal("w1", w1w, w1s)
+        nc.vector.tensor_copy(picked_words[:, halves[1]], xw[:].indirect(offs_sb[:, list_halves[1]]))
+
+        def product(dst, weights, t, words, scales):
+            cols = slice(P * t, P * (t + 1))
+            nc.tensor.matmul_mx(
+                out=dst,
+                lhsT=weights[0][:, cols].bitcast(FP8X4),
+                lhsT_scale=weights[1][:, cols],
+                rhs=words.bitcast(FP8X4),
+                rhs_scale=scales,
+                start=True,
+                stop=True,
+            )
+
+        plus = [sb("plus%d" % t, [P, S], F32) for t in range(PACK)]
+        minus = [sb("minus%d" % t, [P, S], F32) for t in range(PACK)]
+
+        def first_layer(t, cols):
+            y = bank("y", [P, cols.stop - cols.start])
+            product(y[:], w1_dealt, t, picked_words[:, cols], picked_scales[:, cols])
+            nc.scalar.activation(plus[t][:, cols], y[:], COPY, scale=half_gain[:, t : t + 1])
+            nc.scalar.activation(minus[t][:, cols], y[:], COPY, scale=minus_half_gain[:, t : t + 1])
+
+        first_layer(0, halves[0])
+        first_layer(1, halves[0])
+        first_layer(0, halves[1])
+        first_layer(1, halves[1])
+        first_layer(2, slice(0, S))
+        first_layer(3, slice(0, S))
+        w2_dealt = deal("w2", w2w, w2s)
+
+        centre = sb("centre", [P, PACK, S], F32)
+        for t in range(PACK):
+            nc.scalar.activation(centre[:, t, :], plus[t][:], COPY, scale=2.0)
+
+        a = {}
+        b = [sb("b%d" % h, [P, PACK, HALF], F32) for h in range(2)]
+
+        def east_diff(t, h):
+            nc.vector.tensor_tensor(b[h][:, t, :], plus[t][:].indirect(east_sb[:, list_halves[h]]), minus[t][:, halves[h]], ALU.add)
+
+        def west_diff(t, h):
+            if h not in a:
+                a[h] = keep.tile([P, PACK, HALF], F32, name="a%d" % h, tag="a", align_bytes=64)
+            nc.vector.tensor_tensor(a[h][:, t, :], minus[t][:].indirect(west_sb[:, list_halves[h]]), plus[t][:, halves[h]], ALU.add)
+
+        made = {}
+
+        def upper(c0, n):
+            h, lo = divmod(c0, HALF)
+            u = sb("u%d" % c0, [P, PACK, n], F32)
+            nc.vector.scalar_tensor_tensor(u[:], a[h][:, :, lo : lo + n], 0.0, b[h][:, :, lo : lo + n], ALU.max, ALU.min)
+            made["u", c0] = u
+
+        def lower(c0, n):
+            h, lo = divmod(c0, HALF)
+            m = sb("m%d" % c0, [P, PACK, n], F32)
+            nc.vector.scalar_tensor_tensor(m[:], a[h][:, :, lo : lo + n], 0.0, made["u", c0][:], ALU.min, ALU.max)
+            made["m", c0] = m
+
+        def edge(c0, n):
+            z = sb("z%d" % c0, [P, n * PACK], BF16)
+            nc.vector.tensor_tensor(
+                z[:].rearrange("p (c i t) -> p c t i", t=PACK, i=2),
+                made["m", c0][:].rearrange("p t (c i) -> p c t i", i=2),
+                centre[:, :, c0 : c0 + n].rearrange("p t (c i) -> p c t i", i=2),
+                ALU.add,
+            )
+            made["z", c0] = z
+
+        def quantise_z(c0, n):
+            zw = sb("zw%d" % c0, [P, n], U32)
+            zs = sb("zs%d" % c0, [P, n], U8)
+            nc.vector.quantize_mx(out=zw[:].bitcast(FP8X4), scales=zs[:], in_=made["z", c0][:])
+            made["zq", c0] = (zw, zs)
+
+        out_rows = out_0.rearrange("(p t) j -> p t j", t=PACK)
+        out_words = out_1[0].rearrange("p n t -> p (n t)").bitcast(I32)
+        out_scales = sb("out_scales", [P, S], U8)
+
+        def second_layer(c0, n, round_on_vector):
+            zw, zs = made["zq", c0]
+            result = sb("result%d" % c0, [P, PACK, n], F32)
+            rounded = sb("rounded%d" % c0, [P, n, PACK], BF16)
+            for lo in range(0, n, PIECE):
+                cols = slice(lo, lo + PIECE)
+                acc = bank("acc", [P, PACK, PIECE])
+                for t in range(PACK):
+                    product(acc[:, t, :], w2_dealt, t, zw[:, cols], zs[:, cols])
+                if round_on_vector:
+                    nc.vector.tensor_copy(rounded[:, cols, :], acc[:].rearrange("p t n -> p n t"))
+                else:
+                    nc.scalar.copy(rounded[:, cols, :], acc[:].rearrange("p t n -> p n t"))
+                nc.scalar.copy(result[:, :, cols], acc[:])
+            nc.sync.dma_start(out=out_rows[:, :, c0 : c0 + n], in_=result[:])
+            made["r", c0] = rounded
+
+        def quantise_out(c0, n):
+            ow = sb("ow%d" % c0, [P, n], U32)
+            nc.vector.quantize_mx(
+                out=ow[:].bitcast(FP8X4), scales=out_scales[:, c0 : c0 + n], in_=made["r", c0][:].rearrange("p n t -> p (n t)")
+            )
+            nc.sync.dma_start(out=out_words[:, c0 : c0 + n], in_=ow[:].bitcast(I32))
+
+        for t in range(PACK):
+            east_diff(t, 0)
+            west_diff(t, 0)
+        east_diff(0, 1)
+        upper(0, HALF)
+        east_diff(1, 1)
+        lower(0, HALF)
+        east_diff(2, 1)
+        edge(0, HALF)
+        east_diff(3, 1)
+        quantise_z(0, HALF)
+        second_layer(0, HALF, False)
+        for t in range(PACK):
+            west_diff(t, 1)
+        c1, c2 = HALF, HALF + PIECE
+        upper(c1, PIECE)
+        upper(c2, PIECE)
+        lower(c1, PIECE)
+        lower(c2, PIECE)
+        edge(c1, PIECE)
+        quantise_out(0, HALF)
+        quantise_z(c1, PIECE)
+        second_layer(c1, PIECE, False)
+        edge(c2, PIECE)
+        quantise_z(c2, PIECE)
+        quantise_out(c1, PIECE)
+        second_layer(c2, PIECE, True)
+        quantise_out(c2, PIECE)
+        for q in range(4):
+            (nc.sync if q % 2 else nc.scalar).dma_start(
+                out=out_2[0, 4 * q : 4 * q + 4, :].bitcast(I32), in_=out_scales[32 * q : 32 * q + 4, :].bitcast(I32)
+            )

@@ -47,25 +47,25 @@ def tile_picked_minmod_none_po_kernel(
         xw = sb("xw", [P, T], U32)
         xs = sb("xs", [P, T], U8)
         w1w = sb("w1w", [P, H], I32)
-        w1s = sb("w1s", [P, H], U8)
         w2w = sb("w2w", [P, N], I32)
         w2s = sb("w2s", [P, N], U8)
         gain = sb("gain", [P, PACK], F32)
+        w1s = sb("w1s", [P, H], U8)
 
         for plane in (xs, w1s, w2s):
             nc.vector.memset(plane[:].bitcast(I32), 0)
 
-        nc.gpsimd.dma_start(out=gain[:], in_=gn.rearrange("(p t) o -> p (t o)", t=PACK))
+        nc.scalar.dma_start(out=gain[:], in_=gn.rearrange("(p t) o -> p (t o)", t=PACK))
         nc.sync.dma_start(offs_sb[:], offs)
-        nc.sync.dma_start(east_sb[:], east)
-        nc.sync.dma_start(out=xw[:].bitcast(I32), in_=words_of(x_words))
-        for q in range(4):
-            load_scale_rows(nc.sync, xs, x_scales, q)
         nc.sync.dma_start(out=w1w[:], in_=words_of(w1_words))
         for q in range(4):
-            load_scale_rows(nc.sync if q < 2 else nc.gpsimd, w1s, w1_scales, q)
-        nc.sync.dma_start(out=w2w[:], in_=words_of(w2_words))
+            load_scale_rows(nc.sync, xs, x_scales, q)
+        nc.sync.dma_start(out=xw[:].bitcast(I32), in_=words_of(x_words))
+        for q in range(4):
+            load_scale_rows(nc.sync, w1s, w1_scales, q)
+        nc.sync.dma_start(east_sb[:], east)
         nc.sync.dma_start(west_sb[:], west)
+        nc.sync.dma_start(out=w2w[:], in_=words_of(w2_words))
         for q in range(4):
             load_scale_rows(nc.sync, w2s, w2_scales, q)
 
@@ -74,17 +74,18 @@ def tile_picked_minmod_none_po_kernel(
         nc.scalar.activation(half_gain[:], gain[:], COPY, scale=0.5)
         nc.scalar.activation(minus_half_gain[:], gain[:], COPY, scale=-0.5)
 
-        def deal(name, words, scales):
+        def deal(name, words, scales, byte_engine, planes_a_copy):
             dealt_words = sb(name + "_words", [P, 512], I32)
             dealt_scales = sb(name + "_scales", [P, 512], U8)
             nc.vector.tensor_copy(
                 out=dealt_words[:].rearrange("p (t b i) -> p b t i", t=PACK, i=4),
                 in_=words[:].rearrange("p (b i t) -> p b t i", t=PACK, i=4),
             )
-            nc.vector.tensor_copy(
-                out=dealt_scales[:].rearrange("p (t b i) -> p b t i", t=PACK, i=16),
-                in_=scales[:].rearrange("p (b i t) -> p b t i", t=PACK, i=16),
-            )
+            for t in range(0, PACK, planes_a_copy):
+                byte_engine.tensor_copy(
+                    out=dealt_scales[:].rearrange("p (t b i) -> p b t i", t=PACK, i=16)[:, :, t : t + planes_a_copy, :],
+                    in_=scales[:].rearrange("p (b i t) -> p b t i", t=PACK, i=16)[:, :, t : t + planes_a_copy, :],
+                )
             return dealt_words, dealt_scales
 
         picked_scales = sb("picked_scales", [P, S], U8)
@@ -93,7 +94,7 @@ def tile_picked_minmod_none_po_kernel(
         halves = [slice(0, HALF), slice(HALF, S)]
         list_halves = [slice(0, HALF // 16), slice(HALF // 16, S // 16)]
         nc.vector.tensor_copy(picked_words[:, halves[0]], xw[:].indirect(offs_sb[:, list_halves[0]]))
-        w1_dealt = deal("w1", w1w, w1s)
+        w1_dealt = deal("w1", w1w, w1s, nc.gpsimd, 1)
         nc.vector.tensor_copy(picked_words[:, halves[1]], xw[:].indirect(offs_sb[:, list_halves[1]]))
 
         def product(dst, weights, t, words, scales):
@@ -118,12 +119,11 @@ def tile_picked_minmod_none_po_kernel(
             nc.scalar.activation(minus[t][:, cols], y[:], COPY, scale=minus_half_gain[:, t : t + 1])
 
         first_layer(0, halves[0])
-        first_layer(1, halves[0])
         first_layer(0, halves[1])
-        first_layer(1, halves[1])
+        first_layer(1, slice(0, S))
         first_layer(2, slice(0, S))
         first_layer(3, slice(0, S))
-        w2_dealt = deal("w2", w2w, w2s)
+        w2_dealt = deal("w2", w2w, w2s, nc.vector, PACK)
 
         centre = sb("centre", [P, PACK, S], F32)
         for t in range(PACK):
@@ -135,10 +135,13 @@ def tile_picked_minmod_none_po_kernel(
         def east_diff(t, h):
             nc.vector.tensor_tensor(b[h][:, t, :], plus[t][:].indirect(east_sb[:, list_halves[h]]), minus[t][:, halves[h]], ALU.add)
 
-        def west_diff(t, h):
+        def west_diff(t, c0, n):
+            h, lo = divmod(c0, HALF)
             if h not in a:
                 a[h] = keep.tile([P, PACK, HALF], F32, name="a%d" % h, tag="a", align_bytes=64)
-            nc.vector.tensor_tensor(a[h][:, t, :], minus[t][:].indirect(west_sb[:, list_halves[h]]), plus[t][:, halves[h]], ALU.add)
+            nc.vector.tensor_tensor(
+                a[h][:, t, lo : lo + n], minus[t][:].indirect(west_sb[:, c0 // 16 : (c0 + n) // 16]), plus[t][:, c0 : c0 + n], ALU.add
+            )
 
         made = {}
 
@@ -174,20 +177,25 @@ def tile_picked_minmod_none_po_kernel(
         out_words = out_1[0].rearrange("p n t -> p (n t)").bitcast(I32)
         out_scales = sb("out_scales", [P, S], U8)
 
-        def second_layer(c0, n, round_on_vector):
+        def second_layer(c0, n, last):
             zw, zs = made["zq", c0]
             result = sb("result%d" % c0, [P, PACK, n], F32)
             rounded = sb("rounded%d" % c0, [P, n, PACK], BF16)
-            for lo in range(0, n, PIECE):
-                cols = slice(lo, lo + PIECE)
-                acc = bank("acc", [P, PACK, PIECE])
+            if last:
+                for pair in range(0, PACK, 2):
+                    acc = bank("acc", [P, 2, n])
+                    for t in range(2):
+                        product(acc[:, t, :], w2_dealt, pair + t, zw[:], zs[:])
+                    nc.scalar.copy(result[:, pair : pair + 2, :], acc[:])
+                nc.vector.tensor_copy(
+                    rounded[:].rearrange("p (c i) t -> p c t i", i=4), result[:].rearrange("p t (c i) -> p c t i", i=4)
+                )
+            else:
+                acc = bank("acc", [P, PACK, n])
                 for t in range(PACK):
-                    product(acc[:, t, :], w2_dealt, t, zw[:, cols], zs[:, cols])
-                if round_on_vector:
-                    nc.vector.tensor_copy(rounded[:, cols, :], acc[:].rearrange("p t n -> p n t"))
-                else:
-                    nc.scalar.copy(rounded[:, cols, :], acc[:].rearrange("p t n -> p n t"))
-                nc.scalar.copy(result[:, :, cols], acc[:])
+                    product(acc[:, t, :], w2_dealt, t, zw[:], zs[:])
+                nc.scalar.copy(rounded[:], acc[:].rearrange("p t n -> p n t"))
+                nc.scalar.copy(result[:], acc[:])
             nc.sync.dma_start(out=out_rows[:, :, c0 : c0 + n], in_=result[:])
             made["r", c0] = rounded
 
@@ -198,34 +206,38 @@ def tile_picked_minmod_none_po_kernel(
             )
             nc.sync.dma_start(out=out_words[:, c0 : c0 + n], in_=ow[:].bitcast(I32))
 
+        c0, c1, c2, c3 = range(0, S, PIECE)
         for t in range(PACK):
             east_diff(t, 0)
-            west_diff(t, 0)
-        east_diff(0, 1)
-        upper(0, HALF)
-        east_diff(1, 1)
-        lower(0, HALF)
-        east_diff(2, 1)
-        edge(0, HALF)
-        east_diff(3, 1)
-        quantise_z(0, HALF)
-        second_layer(0, HALF, False)
+            west_diff(t, 0, HALF)
         for t in range(PACK):
-            west_diff(t, 1)
-        c1, c2 = HALF, HALF + PIECE
-        upper(c1, PIECE)
-        upper(c2, PIECE)
-        lower(c1, PIECE)
-        lower(c2, PIECE)
+            east_diff(t, 1)
+        for step in (upper, lower):
+            step(c0, PIECE)
+            step(c1, PIECE)
+        edge(c0, PIECE)
+        west_diff(0, c2, PIECE)
+        quantise_z(c0, PIECE)
+        second_layer(c0, PIECE, False)
         edge(c1, PIECE)
-        quantise_out(0, HALF)
+        west_diff(1, c2, PIECE)
         quantise_z(c1, PIECE)
         second_layer(c1, PIECE, False)
-        edge(c2, PIECE)
-        quantise_z(c2, PIECE)
+        west_diff(2, c2, PIECE)
+        west_diff(3, c2, PIECE)
+        for t, step in enumerate((upper, lower, edge, quantise_z)):
+            west_diff(t, c3, PIECE)
+            step(c2, PIECE)
+        second_layer(c2, PIECE, False)
+        upper(c3, PIECE)
+        quantise_out(c0, PIECE)
+        lower(c3, PIECE)
         quantise_out(c1, PIECE)
-        second_layer(c2, PIECE, True)
+        edge(c3, PIECE)
+        quantise_z(c3, PIECE)
         quantise_out(c2, PIECE)
+        second_layer(c3, PIECE, True)
+        quantise_out(c3, PIECE)
         for q in range(4):
             (nc.sync if q % 2 else nc.scalar).dma_start(
                 out=out_2[0, 4 * q : 4 * q + 4, :].bitcast(I32), in_=out_scales[32 * q : 32 * q + 4, :].bitcast(I32)

@@ -1,6 +1,7 @@
 from contextlib import ExitStack
 
 import concourse.mybir as mybir
+from concourse.masks import make_identity
 
 K, T, S, N, H = 512, 2048, 512, 512, 512
 FLOPS = 2 * K * H * S + 2 * H * N * S
@@ -46,7 +47,7 @@ def tile_picked_minmod_none_po_kernel(
         west_sb = keep.tile([P, S // 16], U16, name="west_sb")
         xw = sb("xw", [P, T], U32)
         xs = sb("xs", [P, T], U8)
-        w1w = sb("w1w", [P, H], I32)
+        w1w = keep.tile([P, H], I32, name="w1w", tag="w1w_then_identity", align_bytes=64)
         w2w = sb("w2w", [P, N], I32)
         w2s = sb("w2s", [P, N], U8)
         gain = sb("gain", [P, PACK], F32)
@@ -74,19 +75,26 @@ def tile_picked_minmod_none_po_kernel(
         nc.scalar.activation(half_gain[:], gain[:], COPY, scale=0.5)
         nc.scalar.activation(minus_half_gain[:], gain[:], COPY, scale=-0.5)
 
-        def deal(name, words, scales, byte_engine, planes_a_copy):
-            dealt_words = sb(name + "_words", [P, 512], I32)
-            dealt_scales = sb(name + "_scales", [P, 512], U8)
+        def deal_words(name, words):
+            dealt = sb(name + "_words", [P, 512], I32)
             nc.vector.tensor_copy(
-                out=dealt_words[:].rearrange("p (t b i) -> p b t i", t=PACK, i=4),
+                out=dealt[:].rearrange("p (t b i) -> p b t i", t=PACK, i=4),
                 in_=words[:].rearrange("p (b i t) -> p b t i", t=PACK, i=4),
             )
+            return dealt
+
+        def deal_scales(name, scales, engine, planes_a_copy):
+            dealt = sb(name + "_scales", [P, 512], U8)
             for t in range(0, PACK, planes_a_copy):
-                byte_engine.tensor_copy(
-                    out=dealt_scales[:].rearrange("p (t b i) -> p b t i", t=PACK, i=16)[:, :, t : t + planes_a_copy, :],
+                engine.tensor_copy(
+                    out=dealt[:].rearrange("p (t b i) -> p b t i", t=PACK, i=16)[:, :, t : t + planes_a_copy, :],
                     in_=scales[:].rearrange("p (b i t) -> p b t i", t=PACK, i=16)[:, :, t : t + planes_a_copy, :],
                 )
-            return dealt_words, dealt_scales
+            return dealt
+
+        w1_dealt_words = deal_words("w1", w1w)
+        identity = keep.tile([P, P], F32, name="identity", tag="w1w_then_identity", align_bytes=64)
+        make_identity(nc, identity[:])
 
         picked_scales = sb("picked_scales", [P, S], U8)
         picked_words = sb("picked_words", [P, S], U32)
@@ -94,7 +102,7 @@ def tile_picked_minmod_none_po_kernel(
         halves = [slice(0, HALF), slice(HALF, S)]
         list_halves = [slice(0, HALF // 16), slice(HALF // 16, S // 16)]
         nc.vector.tensor_copy(picked_words[:, halves[0]], xw[:].indirect(offs_sb[:, list_halves[0]]))
-        w1_dealt = deal("w1", w1w, w1s, nc.gpsimd, 1)
+        w1_dealt = (w1_dealt_words, deal_scales("w1", w1s, nc.gpsimd, 1))
         nc.vector.tensor_copy(picked_words[:, halves[1]], xw[:].indirect(offs_sb[:, list_halves[1]]))
 
         def product(dst, weights, t, words, scales):
@@ -112,49 +120,76 @@ def tile_picked_minmod_none_po_kernel(
         plus = [sb("plus%d" % t, [P, S], F32) for t in range(PACK)]
         minus = [sb("minus%d" % t, [P, S], F32) for t in range(PACK)]
 
-        def first_layer(t, cols):
+        def first_layer(t, cols, plus_on_vector=False):
             y = bank("y", [P, cols.stop - cols.start])
             product(y[:], w1_dealt, t, picked_words[:, cols], picked_scales[:, cols])
-            nc.scalar.activation(plus[t][:, cols], y[:], COPY, scale=half_gain[:, t : t + 1])
+            if plus_on_vector:
+                nc.vector.tensor_scalar(plus[t][:, cols], y[:], half_gain[:, t : t + 1], None, ALU.mult)
+            else:
+                nc.scalar.activation(plus[t][:, cols], y[:], COPY, scale=half_gain[:, t : t + 1])
             nc.scalar.activation(minus[t][:, cols], y[:], COPY, scale=minus_half_gain[:, t : t + 1])
 
         first_layer(0, halves[0])
-        first_layer(0, halves[1])
+        first_layer(0, halves[1], True)
         first_layer(1, slice(0, S))
         first_layer(2, slice(0, S))
         first_layer(3, slice(0, S))
-        w2_dealt = deal("w2", w2w, w2s, nc.vector, PACK)
+        w2_dealt = (deal_words("w2", w2w), deal_scales("w2", w2s, nc.vector, PACK))
 
-        centre = sb("centre", [P, PACK, S], F32)
+        def add_transposed(dst, src, start, stop):
+            nc.tensor.matmul(dst, src, identity[:], is_transpose=True, start=start, stop=stop)
+
+        turned = {}
+        for c0 in range(0, HALF, PIECE):
+            turned[c0] = bank("turned", [P, PACK, P])
+            for t in range(PACK):
+                for again in range(2):
+                    add_transposed(turned[c0][:, t, :], plus[t][:, c0 : c0 + PIECE], t == 0 and again == 0, False)
+
+        centre = sb("centre", [P, PACK, HALF], F32)
         for t in range(PACK):
-            nc.scalar.activation(centre[:, t, :], plus[t][:], COPY, scale=2.0)
+            nc.scalar.activation(centre[:, t, :], plus[t][:, halves[1]], COPY, scale=2.0)
 
         a = {}
-        b = [sb("b%d" % h, [P, PACK, HALF], F32) for h in range(2)]
+        b = {}
 
-        def east_diff(t, h):
-            nc.vector.tensor_tensor(b[h][:, t, :], plus[t][:].indirect(east_sb[:, list_halves[h]]), minus[t][:, halves[h]], ALU.add)
+        b_rows = sb("b_rows", [P, PACK + 1, HALF], F32)
+        for c0 in range(0, S, PIECE):
+            first = 1 if c0 < HALF else 0
+            b[c0] = b_rows[:, first : first + PACK, c0 % HALF : c0 % HALF + PIECE]
+
+        def east_diff(t, c0, n):
+            nc.vector.tensor_tensor(
+                b_rows[:, t + (1 if c0 < HALF else 0), :],
+                plus[t][:].indirect(east_sb[:, c0 // 16 : (c0 + n) // 16]),
+                minus[t][:, c0 : c0 + n],
+                ALU.add,
+            )
 
         def west_diff(t, c0, n):
-            h, lo = divmod(c0, HALF)
-            if h not in a:
-                a[h] = keep.tile([P, PACK, HALF], F32, name="a%d" % h, tag="a", align_bytes=64)
+            h0 = c0 - c0 % HALF
+            if h0 not in a:
+                tile = keep.tile([P, PACK, HALF], F32, name="a%d" % h0, tag="a", align_bytes=64)
+                for lo in range(0, HALF, PIECE):
+                    a[h0 + lo] = tile[:, :, lo : lo + PIECE]
+                a["whole", h0] = tile
             nc.vector.tensor_tensor(
-                a[h][:, t, lo : lo + n], minus[t][:].indirect(west_sb[:, c0 // 16 : (c0 + n) // 16]), plus[t][:, c0 : c0 + n], ALU.add
+                a["whole", h0][:, t, c0 - h0 : c0 - h0 + n],
+                minus[t][:].indirect(west_sb[:, c0 // 16 : (c0 + n) // 16]),
+                plus[t][:, c0 : c0 + n],
+                ALU.add,
             )
 
         made = {}
 
         def upper(c0, n):
-            h, lo = divmod(c0, HALF)
-            u = sb("u%d" % c0, [P, PACK, n], F32)
-            nc.vector.scalar_tensor_tensor(u[:], a[h][:, :, lo : lo + n], 0.0, b[h][:, :, lo : lo + n], ALU.max, ALU.min)
+            u = keep.tile([P, PACK, n], F32, name="u%d" % c0, align_bytes=64)
+            nc.vector.scalar_tensor_tensor(u[:], a[c0], 0.0, b[c0], ALU.max, ALU.min)
             made["u", c0] = u
 
         def lower(c0, n):
-            h, lo = divmod(c0, HALF)
-            m = sb("m%d" % c0, [P, PACK, n], F32)
-            nc.vector.scalar_tensor_tensor(m[:], a[h][:, :, lo : lo + n], 0.0, made["u", c0][:], ALU.min, ALU.max)
+            m = keep.tile([P, PACK, n], F32, name="m%d" % c0, align_bytes=64)
+            nc.vector.scalar_tensor_tensor(m[:], a[c0], 0.0, made["u", c0][:], ALU.min, ALU.max)
             made["m", c0] = m
 
         def edge(c0, n):
@@ -162,9 +197,21 @@ def tile_picked_minmod_none_po_kernel(
             nc.vector.tensor_tensor(
                 z[:].rearrange("p (c i t) -> p c t i", t=PACK, i=2),
                 made["m", c0][:].rearrange("p t (c i) -> p c t i", i=2),
-                centre[:, :, c0 : c0 + n].rearrange("p t (c i) -> p c t i", i=2),
+                centre[:, :, c0 - HALF : c0 - HALF + n].rearrange("p t (c i) -> p c t i", i=2),
                 ALU.add,
             )
+            made["z", c0] = z
+
+        def edge_on_tensor(c0):
+            for t in range(PACK):
+                add_transposed(turned[c0][:, t, :], made["m", c0][:, t, :], False, t == PACK - 1)
+            pairs = sb("pairs%d" % c0, [P, 2, P, 2], BF16)
+            nc.scalar.copy(pairs[:], turned[c0][:].rearrange("j (u e) p -> j u p e", e=2))
+            back = bank("back", [P, 2, P])
+            for u in range(2):
+                nc.tensor.transpose(back[:, u, :], pairs[:, u, :, :].rearrange("j p e -> j (p e)").bitcast(F32), identity[:])
+            z = keep.tile([P, PIECE * PACK], BF16, name="z%d" % c0, align_bytes=64)
+            nc.scalar.copy(z[:].bitcast(F32).rearrange("p (j u) -> p j u", u=2), back[:].rearrange("p u j -> p j u"))
             made["z", c0] = z
 
         def quantise_z(c0, n):
@@ -199,27 +246,33 @@ def tile_picked_minmod_none_po_kernel(
             nc.sync.dma_start(out=out_rows[:, :, c0 : c0 + n], in_=result[:])
             made["r", c0] = rounded
 
+        out_codes = sb("out_codes", [P, S], U32)
+
         def quantise_out(c0, n):
-            ow = sb("ow%d" % c0, [P, n], U32)
             nc.vector.quantize_mx(
-                out=ow[:].bitcast(FP8X4), scales=out_scales[:, c0 : c0 + n], in_=made["r", c0][:].rearrange("p n t -> p (n t)")
+                out=out_codes[:, c0 : c0 + n].bitcast(FP8X4),
+                scales=out_scales[:, c0 : c0 + n],
+                in_=made["r", c0][:].rearrange("p n t -> p (n t)"),
             )
-            nc.sync.dma_start(out=out_words[:, c0 : c0 + n], in_=ow[:].bitcast(I32))
+
+        def store_codes(cols):
+            nc.sync.dma_start(out=out_words[:, cols], in_=out_codes[:, cols].bitcast(I32))
 
         c0, c1, c2, c3 = range(0, S, PIECE)
         for t in range(PACK):
-            east_diff(t, 0)
+            east_diff(t, 0, HALF)
             west_diff(t, 0, HALF)
+        upper(c0, PIECE)
+        upper(c1, PIECE)
+        lower(c0, PIECE)
+        lower(c1, PIECE)
+        edge_on_tensor(c0)
+        edge_on_tensor(c1)
         for t in range(PACK):
-            east_diff(t, 1)
-        for step in (upper, lower):
-            step(c0, PIECE)
-            step(c1, PIECE)
-        edge(c0, PIECE)
-        west_diff(0, c2, PIECE)
+            east_diff(t, HALF, HALF)
         quantise_z(c0, PIECE)
         second_layer(c0, PIECE, False)
-        edge(c1, PIECE)
+        west_diff(0, c2, PIECE)
         west_diff(1, c2, PIECE)
         quantise_z(c1, PIECE)
         second_layer(c1, PIECE, False)
@@ -236,8 +289,10 @@ def tile_picked_minmod_none_po_kernel(
         edge(c3, PIECE)
         quantise_z(c3, PIECE)
         quantise_out(c2, PIECE)
+        store_codes(slice(0, c3))
         second_layer(c3, PIECE, True)
         quantise_out(c3, PIECE)
+        store_codes(slice(c3, S))
         for q in range(4):
             (nc.sync if q % 2 else nc.scalar).dma_start(
                 out=out_2[0, 4 * q : 4 * q + 4, :].bitcast(I32), in_=out_scales[32 * q : 32 * q + 4, :].bitcast(I32)

@@ -18,8 +18,12 @@ COPY = mybir.ActivationFunctionType.Copy
 
 P = 128
 PACK = 4
+QUADRANTS = 4
+GROUP = 16
 HALF = S // 2
 PIECE = 128
+PSUM_BANKS = 8
+X_AHEAD = T // 4
 
 
 def tile_picked_minmod_none_po_kernel(
@@ -28,10 +32,10 @@ def tile_picked_minmod_none_po_kernel(
     nc = tc.nc
     with ExitStack() as ctx:
         keep = ctx.enter_context(tc.tile_pool(name="keep", bufs=1))
-        psum = ctx.enter_context(tc.psum_pool(name="psum", bufs=8))
+        psum = ctx.enter_context(tc.psum_pool(name="psum", bufs=PSUM_BANKS))
 
-        def sb(name, shape, dtype):
-            return keep.tile(shape, dtype, name=name, align_bytes=64)
+        def sb(name, shape, dtype, tag=""):
+            return keep.tile(shape, dtype, name=name, tag=tag, align_bytes=64)
 
         def bank(name, shape):
             return psum.tile(shape, F32, name=name, tag="bank")
@@ -39,36 +43,38 @@ def tile_picked_minmod_none_po_kernel(
         def words_of(dram):
             return dram[0].rearrange("p n t -> p (n t)").bitcast(I32)
 
-        def load_scale_rows(queue, tile, dram, q):
-            queue.dma_start(out=tile[32 * q : 32 * q + 4, :].bitcast(I32), in_=dram[0, 4 * q : 4 * q + 4, :].bitcast(I32))
+        def load_scale_rows(tile, dram):
+            for q in range(QUADRANTS):
+                nc.sync.dma_start(out=tile[32 * q : 32 * q + 4, :].bitcast(I32), in_=dram[0, 4 * q : 4 * q + 4, :].bitcast(I32))
 
-        offs_sb = keep.tile([P, S // 16], U16, name="offs_sb")
-        east_sb = keep.tile([P, S // 16], U16, name="east_sb")
-        west_sb = keep.tile([P, S // 16], U16, name="west_sb")
+        def entries(list_tile, c0, n):
+            return list_tile[:, c0 // GROUP : (c0 + n) // GROUP]
+
+        offs_sb = keep.tile([P, S // GROUP], U16, name="offs_sb")
+        east_sb = keep.tile([P, S // GROUP], U16, name="east_sb")
+        west_sb = keep.tile([P, S // GROUP], U16, name="west_sb")
         xw = sb("xw", [P, T], U32)
         xs = sb("xs", [P, T], U8)
-        w1w = keep.tile([P, H], I32, name="w1w", tag="w1w_then_identity", align_bytes=64)
+        w1w = sb("w1w", [P, H], I32, tag="w1w_then_identity")
         w2w = sb("w2w", [P, N], I32)
         w2s = sb("w2s", [P, N], U8)
         gain = sb("gain", [P, PACK], F32)
         w1s = sb("w1s", [P, H], U8)
 
-        for plane in (xs, w1s, w2s):
-            nc.vector.memset(plane[:].bitcast(I32), 0)
+        for scale_tile in (xs, w1s, w2s):
+            nc.vector.memset(scale_tile[:].bitcast(I32), 0)
 
-        nc.scalar.dma_start(out=gain[:], in_=gn.rearrange("(p t) o -> p (t o)", t=PACK))
         nc.sync.dma_start(offs_sb[:], offs)
         nc.sync.dma_start(out=w1w[:], in_=words_of(w1_words))
-        for q in range(4):
-            load_scale_rows(nc.sync, xs, x_scales, q)
-        nc.sync.dma_start(out=xw[:].bitcast(I32), in_=words_of(x_words))
-        for q in range(4):
-            load_scale_rows(nc.sync, w1s, w1_scales, q)
+        nc.sync.dma_start(out=xw[:, :X_AHEAD].bitcast(I32), in_=words_of(x_words)[:, :X_AHEAD])
+        load_scale_rows(xs, x_scales)
+        nc.sync.dma_start(out=xw[:, X_AHEAD:].bitcast(I32), in_=words_of(x_words)[:, X_AHEAD:])
+        load_scale_rows(w1s, w1_scales)
+        nc.sync.dma_start(out=gain[:], in_=gn.rearrange("(p t) o -> p (t o)", t=PACK))
+        nc.sync.dma_start(out=w2w[:], in_=words_of(w2_words))
         nc.sync.dma_start(east_sb[:], east)
         nc.sync.dma_start(west_sb[:], west)
-        nc.sync.dma_start(out=w2w[:], in_=words_of(w2_words))
-        for q in range(4):
-            load_scale_rows(nc.sync, w2s, w2_scales, q)
+        load_scale_rows(w2s, w2_scales)
 
         half_gain = sb("half_gain", [P, PACK], F32)
         minus_half_gain = sb("minus_half_gain", [P, PACK], F32)
@@ -76,7 +82,7 @@ def tile_picked_minmod_none_po_kernel(
         nc.scalar.activation(minus_half_gain[:], gain[:], COPY, scale=-0.5)
 
         def deal_words(name, words):
-            dealt = sb(name + "_words", [P, 512], I32)
+            dealt = sb(name + "_words", [P, PACK * P], I32)
             nc.vector.tensor_copy(
                 out=dealt[:].rearrange("p (t b i) -> p b t i", t=PACK, i=4),
                 in_=words[:].rearrange("p (b i t) -> p b t i", t=PACK, i=4),
@@ -84,7 +90,7 @@ def tile_picked_minmod_none_po_kernel(
             return dealt
 
         def deal_scales(name, scales, engine, planes_a_copy):
-            dealt = sb(name + "_scales", [P, 512], U8)
+            dealt = sb(name + "_scales", [P, PACK * P], U8)
             for t in range(0, PACK, planes_a_copy):
                 engine.tensor_copy(
                     out=dealt[:].rearrange("p (t b i) -> p b t i", t=PACK, i=16)[:, :, t : t + planes_a_copy, :],
@@ -93,17 +99,16 @@ def tile_picked_minmod_none_po_kernel(
             return dealt
 
         w1_dealt_words = deal_words("w1", w1w)
-        identity = keep.tile([P, P], F32, name="identity", tag="w1w_then_identity", align_bytes=64)
+        identity = sb("identity", [P, P], F32, tag="w1w_then_identity")
         make_identity(nc, identity[:])
 
         picked_scales = sb("picked_scales", [P, S], U8)
         picked_words = sb("picked_words", [P, S], U32)
+        first_half, second_half, all_columns = slice(0, HALF), slice(HALF, S), slice(0, S)
         nc.vector.tensor_copy(picked_scales[:], xs[:].indirect(offs_sb[:]))
-        halves = [slice(0, HALF), slice(HALF, S)]
-        list_halves = [slice(0, HALF // 16), slice(HALF // 16, S // 16)]
-        nc.vector.tensor_copy(picked_words[:, halves[0]], xw[:].indirect(offs_sb[:, list_halves[0]]))
+        nc.vector.tensor_copy(picked_words[:, first_half], xw[:].indirect(entries(offs_sb, 0, HALF)))
         w1_dealt = (w1_dealt_words, deal_scales("w1", w1s, nc.gpsimd, 1))
-        nc.vector.tensor_copy(picked_words[:, halves[1]], xw[:].indirect(offs_sb[:, list_halves[1]]))
+        nc.vector.tensor_copy(picked_words[:, second_half], xw[:].indirect(entries(offs_sb, HALF, HALF)))
 
         def product(dst, weights, t, words, scales):
             cols = slice(P * t, P * (t + 1))
@@ -120,7 +125,7 @@ def tile_picked_minmod_none_po_kernel(
         plus = [sb("plus%d" % t, [P, S], F32) for t in range(PACK)]
         minus = [sb("minus%d" % t, [P, S], F32) for t in range(PACK)]
 
-        def first_layer(t, cols, plus_on_vector=False):
+        def first_layer(t, cols, plus_on_vector):
             y = bank("y", [P, cols.stop - cols.start])
             product(y[:], w1_dealt, t, picked_words[:, cols], picked_scales[:, cols])
             if plus_on_vector:
@@ -129,11 +134,10 @@ def tile_picked_minmod_none_po_kernel(
                 nc.scalar.activation(plus[t][:, cols], y[:], COPY, scale=half_gain[:, t : t + 1])
             nc.scalar.activation(minus[t][:, cols], y[:], COPY, scale=minus_half_gain[:, t : t + 1])
 
-        first_layer(0, halves[0])
-        first_layer(0, halves[1], True)
-        first_layer(1, slice(0, S))
-        first_layer(2, slice(0, S))
-        first_layer(3, slice(0, S))
+        first_layer(0, first_half, False)
+        first_layer(0, second_half, True)
+        for t in range(1, PACK):
+            first_layer(t, all_columns, False)
         w2_dealt = (deal_words("w2", w2w), deal_scales("w2", w2s, nc.vector, PACK))
 
         def add_transposed(dst, src, start, stop):
@@ -143,94 +147,85 @@ def tile_picked_minmod_none_po_kernel(
         for c0 in range(0, HALF, PIECE):
             turned[c0] = bank("turned", [P, PACK, P])
             for t in range(PACK):
-                for again in range(2):
-                    add_transposed(turned[c0][:, t, :], plus[t][:, c0 : c0 + PIECE], t == 0 and again == 0, False)
+                add_transposed(turned[c0][:, t, :], plus[t][:, c0 : c0 + PIECE], t == 0, False)
+                add_transposed(turned[c0][:, t, :], plus[t][:, c0 : c0 + PIECE], False, False)
 
         centre = sb("centre", [P, PACK, HALF], F32)
         for t in range(PACK):
-            nc.scalar.activation(centre[:, t, :], plus[t][:, halves[1]], COPY, scale=2.0)
-
-        a = {}
-        b = {}
+            nc.scalar.activation(centre[:, t, :], plus[t][:, second_half], COPY, scale=2.0)
 
         b_rows = sb("b_rows", [P, PACK + 1, HALF], F32)
-        for c0 in range(0, S, PIECE):
-            first = 1 if c0 < HALF else 0
-            b[c0] = b_rows[:, first : first + PACK, c0 % HALF : c0 % HALF + PIECE]
+        a_half = {}
+
+        def b_planes(c0):
+            first_row = 1 if c0 < HALF else 0
+            return b_rows[:, first_row : first_row + PACK, :]
+
+        def a_planes(c0):
+            h0 = c0 - c0 % HALF
+            if h0 not in a_half:
+                a_half[h0] = sb("a%d" % h0, [P, PACK, HALF], F32, tag="a")
+            return a_half[h0]
+
+        def in_half(c0, n):
+            return slice(c0 % HALF, c0 % HALF + n)
 
         def east_diff(t, c0, n):
             nc.vector.tensor_tensor(
-                b_rows[:, t + (1 if c0 < HALF else 0), :],
-                plus[t][:].indirect(east_sb[:, c0 // 16 : (c0 + n) // 16]),
-                minus[t][:, c0 : c0 + n],
-                ALU.add,
+                b_planes(c0)[:, t, in_half(c0, n)], plus[t][:].indirect(entries(east_sb, c0, n)), minus[t][:, c0 : c0 + n], ALU.add
             )
 
         def west_diff(t, c0, n):
-            h0 = c0 - c0 % HALF
-            if h0 not in a:
-                tile = keep.tile([P, PACK, HALF], F32, name="a%d" % h0, tag="a", align_bytes=64)
-                for lo in range(0, HALF, PIECE):
-                    a[h0 + lo] = tile[:, :, lo : lo + PIECE]
-                a["whole", h0] = tile
             nc.vector.tensor_tensor(
-                a["whole", h0][:, t, c0 - h0 : c0 - h0 + n],
-                minus[t][:].indirect(west_sb[:, c0 // 16 : (c0 + n) // 16]),
-                plus[t][:, c0 : c0 + n],
-                ALU.add,
+                a_planes(c0)[:, t, in_half(c0, n)], minus[t][:].indirect(entries(west_sb, c0, n)), plus[t][:, c0 : c0 + n], ALU.add
             )
 
-        made = {}
+        capped, limited, z_bf16, z_mx, out_bf16 = {}, {}, {}, {}, {}
 
-        def upper(c0, n):
-            u = keep.tile([P, PACK, n], F32, name="u%d" % c0, align_bytes=64)
-            nc.vector.scalar_tensor_tensor(u[:], a[c0], 0.0, b[c0], ALU.max, ALU.min)
-            made["u", c0] = u
+        def cap(c0):
+            capped[c0] = sb("u%d" % c0, [P, PACK, PIECE], F32)
+            cols = in_half(c0, PIECE)
+            nc.vector.scalar_tensor_tensor(capped[c0][:], a_planes(c0)[:, :, cols], 0.0, b_planes(c0)[:, :, cols], ALU.max, ALU.min)
 
-        def lower(c0, n):
-            m = keep.tile([P, PACK, n], F32, name="m%d" % c0, align_bytes=64)
-            nc.vector.scalar_tensor_tensor(m[:], a[c0], 0.0, made["u", c0][:], ALU.min, ALU.max)
-            made["m", c0] = m
+        def limit(c0):
+            limited[c0] = sb("m%d" % c0, [P, PACK, PIECE], F32)
+            nc.vector.scalar_tensor_tensor(limited[c0][:], a_planes(c0)[:, :, in_half(c0, PIECE)], 0.0, capped[c0][:], ALU.min, ALU.max)
 
-        def edge(c0, n):
-            z = sb("z%d" % c0, [P, n * PACK], BF16)
+        def edge_on_vector(c0):
+            z_bf16[c0] = sb("z%d" % c0, [P, PIECE * PACK], BF16)
             nc.vector.tensor_tensor(
-                z[:].rearrange("p (c i t) -> p c t i", t=PACK, i=2),
-                made["m", c0][:].rearrange("p t (c i) -> p c t i", i=2),
-                centre[:, :, c0 - HALF : c0 - HALF + n].rearrange("p t (c i) -> p c t i", i=2),
+                z_bf16[c0][:].rearrange("p (c i t) -> p c t i", t=PACK, i=2),
+                limited[c0][:].rearrange("p t (c i) -> p c t i", i=2),
+                centre[:, :, in_half(c0, PIECE)].rearrange("p t (c i) -> p c t i", i=2),
                 ALU.add,
             )
-            made["z", c0] = z
 
         def edge_on_tensor(c0):
             for t in range(PACK):
-                add_transposed(turned[c0][:, t, :], made["m", c0][:, t, :], False, t == PACK - 1)
+                add_transposed(turned[c0][:, t, :], limited[c0][:, t, :], False, t == PACK - 1)
             pairs = sb("pairs%d" % c0, [P, 2, P, 2], BF16)
             nc.scalar.copy(pairs[:], turned[c0][:].rearrange("j (u e) p -> j u p e", e=2))
             back = bank("back", [P, 2, P])
             for u in range(2):
                 nc.tensor.transpose(back[:, u, :], pairs[:, u, :, :].rearrange("j p e -> j (p e)").bitcast(F32), identity[:])
-            z = keep.tile([P, PIECE * PACK], BF16, name="z%d" % c0, align_bytes=64)
-            nc.scalar.copy(z[:].bitcast(F32).rearrange("p (j u) -> p j u", u=2), back[:].rearrange("p u j -> p j u"))
-            made["z", c0] = z
+            z_bf16[c0] = sb("z%d" % c0, [P, PIECE * PACK], BF16)
+            nc.scalar.copy(z_bf16[c0][:].bitcast(F32).rearrange("p (j u) -> p j u", u=2), back[:].rearrange("p u j -> p j u"))
 
-        def quantise_z(c0, n):
-            zw = sb("zw%d" % c0, [P, n], U32)
-            zs = sb("zs%d" % c0, [P, n], U8)
-            nc.vector.quantize_mx(out=zw[:].bitcast(FP8X4), scales=zs[:], in_=made["z", c0][:])
-            made["zq", c0] = (zw, zs)
+        def quantise_z(c0):
+            z_mx[c0] = (sb("zw%d" % c0, [P, PIECE], U32), sb("zs%d" % c0, [P, PIECE], U8))
+            nc.vector.quantize_mx(out=z_mx[c0][0][:].bitcast(FP8X4), scales=z_mx[c0][1][:], in_=z_bf16[c0][:])
 
         out_rows = out_0.rearrange("(p t) j -> p t j", t=PACK)
         out_words = out_1[0].rearrange("p n t -> p (n t)").bitcast(I32)
         out_scales = sb("out_scales", [P, S], U8)
 
-        def second_layer(c0, n, last):
-            zw, zs = made["zq", c0]
-            result = sb("result%d" % c0, [P, PACK, n], F32)
-            rounded = sb("rounded%d" % c0, [P, n, PACK], BF16)
-            if last:
+        def second_layer(c0):
+            zw, zs = z_mx[c0]
+            result = sb("result%d" % c0, [P, PACK, PIECE], F32)
+            rounded = sb("rounded%d" % c0, [P, PIECE, PACK], BF16)
+            if c0 == S - PIECE:
                 for pair in range(0, PACK, 2):
-                    acc = bank("acc", [P, 2, n])
+                    acc = bank("acc", [P, 2, PIECE])
                     for t in range(2):
                         product(acc[:, t, :], w2_dealt, pair + t, zw[:], zs[:])
                     nc.scalar.copy(result[:, pair : pair + 2, :], acc[:])
@@ -238,62 +233,56 @@ def tile_picked_minmod_none_po_kernel(
                     rounded[:].rearrange("p (c i) t -> p c t i", i=4), result[:].rearrange("p t (c i) -> p c t i", i=4)
                 )
             else:
-                acc = bank("acc", [P, PACK, n])
+                acc = bank("acc", [P, PACK, PIECE])
                 for t in range(PACK):
                     product(acc[:, t, :], w2_dealt, t, zw[:], zs[:])
                 nc.scalar.copy(rounded[:], acc[:].rearrange("p t n -> p n t"))
                 nc.scalar.copy(result[:], acc[:])
-            nc.sync.dma_start(out=out_rows[:, :, c0 : c0 + n], in_=result[:])
-            made["r", c0] = rounded
+            nc.sync.dma_start(out=out_rows[:, :, c0 : c0 + PIECE], in_=result[:])
+            out_bf16[c0] = rounded
 
         out_codes = sb("out_codes", [P, S], U32)
 
-        def quantise_out(c0, n):
+        def quantise_out(c0):
             nc.vector.quantize_mx(
-                out=out_codes[:, c0 : c0 + n].bitcast(FP8X4),
-                scales=out_scales[:, c0 : c0 + n],
-                in_=made["r", c0][:].rearrange("p n t -> p (n t)"),
+                out=out_codes[:, c0 : c0 + PIECE].bitcast(FP8X4),
+                scales=out_scales[:, c0 : c0 + PIECE],
+                in_=out_bf16[c0][:].rearrange("p n t -> p (n t)"),
             )
 
         def store_codes(cols):
             nc.sync.dma_start(out=out_words[:, cols], in_=out_codes[:, cols].bitcast(I32))
 
-        c0, c1, c2, c3 = range(0, S, PIECE)
+        piece0, piece1, piece2, piece3 = range(0, S, PIECE)
         for t in range(PACK):
             east_diff(t, 0, HALF)
             west_diff(t, 0, HALF)
-        upper(c0, PIECE)
-        upper(c1, PIECE)
-        lower(c0, PIECE)
-        lower(c1, PIECE)
-        edge_on_tensor(c0)
-        edge_on_tensor(c1)
+        for step in (cap, limit, edge_on_tensor):
+            step(piece0)
+            step(piece1)
         for t in range(PACK):
             east_diff(t, HALF, HALF)
-        quantise_z(c0, PIECE)
-        second_layer(c0, PIECE, False)
-        west_diff(0, c2, PIECE)
-        west_diff(1, c2, PIECE)
-        quantise_z(c1, PIECE)
-        second_layer(c1, PIECE, False)
-        west_diff(2, c2, PIECE)
-        west_diff(3, c2, PIECE)
-        for t, step in enumerate((upper, lower, edge, quantise_z)):
-            west_diff(t, c3, PIECE)
-            step(c2, PIECE)
-        second_layer(c2, PIECE, False)
-        upper(c3, PIECE)
-        quantise_out(c0, PIECE)
-        lower(c3, PIECE)
-        quantise_out(c1, PIECE)
-        edge(c3, PIECE)
-        quantise_z(c3, PIECE)
-        quantise_out(c2, PIECE)
-        store_codes(slice(0, c3))
-        second_layer(c3, PIECE, True)
-        quantise_out(c3, PIECE)
-        store_codes(slice(c3, S))
-        for q in range(4):
+        for piece, planes in ((piece0, (0, 1)), (piece1, (2, 3))):
+            quantise_z(piece)
+            second_layer(piece)
+            for t in planes:
+                west_diff(t, piece2, PIECE)
+        for t, step in enumerate((cap, limit, edge_on_vector, quantise_z)):
+            west_diff(t, piece3, PIECE)
+            step(piece2)
+        second_layer(piece2)
+        cap(piece3)
+        quantise_out(piece0)
+        limit(piece3)
+        quantise_out(piece1)
+        edge_on_vector(piece3)
+        quantise_z(piece3)
+        quantise_out(piece2)
+        store_codes(slice(0, piece3))
+        second_layer(piece3)
+        quantise_out(piece3)
+        store_codes(slice(piece3, S))
+        for q in range(QUADRANTS):
             (nc.sync if q % 2 else nc.scalar).dma_start(
                 out=out_2[0, 4 * q : 4 * q + 4, :].bitcast(I32), in_=out_scales[32 * q : 32 * q + 4, :].bitcast(I32)
             )

@@ -23,7 +23,7 @@ GROUP = 16
 HALF = S // 2
 PIECE = 128
 PSUM_BANKS = 8
-X_AHEAD = T // 4
+X_AHEAD = 3 * T // 8
 
 
 def tile_picked_minmod_none_po_kernel(
@@ -55,20 +55,21 @@ def tile_picked_minmod_none_po_kernel(
         west_sb = keep.tile([P, S // GROUP], U16, name="west_sb")
         xw = sb("xw", [P, T], U32)
         xs = sb("xs", [P, T], U8)
-        w1w = sb("w1w", [P, H], I32, tag="w1w_then_identity")
+        w1w = sb("w1w", [P, H], I32)
         w2w = sb("w2w", [P, N], I32)
         w2s = sb("w2s", [P, N], U8)
         gain = sb("gain", [P, PACK], F32)
         w1s = sb("w1s", [P, H], U8)
 
-        for scale_tile in (xs, w1s, w2s):
-            nc.vector.memset(scale_tile[:].bitcast(I32), 0)
+        nc.vector.memset(xs[:].bitcast(I32), 0)
+        for scale_tile in (w1s, w2s):
+            nc.gpsimd.memset(scale_tile[:].bitcast(I32), 0)
 
-        nc.sync.dma_start(offs_sb[:], offs)
-        nc.sync.dma_start(out=w1w[:], in_=words_of(w1_words))
         nc.sync.dma_start(out=xw[:, :X_AHEAD].bitcast(I32), in_=words_of(x_words)[:, :X_AHEAD])
+        nc.sync.dma_start(offs_sb[:], offs)
         load_scale_rows(xs, x_scales)
         nc.sync.dma_start(out=xw[:, X_AHEAD:].bitcast(I32), in_=words_of(x_words)[:, X_AHEAD:])
+        nc.sync.dma_start(out=w1w[:], in_=words_of(w1_words))
         load_scale_rows(w1s, w1_scales)
         nc.sync.dma_start(out=gain[:], in_=gn.rearrange("(p t) o -> p (t o)", t=PACK))
         nc.sync.dma_start(out=w2w[:], in_=words_of(w2_words))
@@ -81,25 +82,19 @@ def tile_picked_minmod_none_po_kernel(
         nc.scalar.activation(half_gain[:], gain[:], COPY, scale=0.5)
         nc.scalar.activation(minus_half_gain[:], gain[:], COPY, scale=-0.5)
 
-        def deal_words(name, words):
-            dealt = sb(name + "_words", [P, PACK * P], I32)
+        def deal(dealt, source, run, planes):
             nc.vector.tensor_copy(
-                out=dealt[:].rearrange("p (t b i) -> p b t i", t=PACK, i=4),
-                in_=words[:].rearrange("p (b i t) -> p b t i", t=PACK, i=4),
+                out=dealt[:].rearrange("p (t b i) -> p b t i", t=PACK, i=run)[:, :, planes, :],
+                in_=source[:].rearrange("p (b i t) -> p b t i", t=PACK, i=run)[:, :, planes, :],
             )
-            return dealt
 
-        def deal_scales(name, scales, engine, planes_a_copy):
-            dealt = sb(name + "_scales", [P, PACK * P], U8)
-            for t in range(0, PACK, planes_a_copy):
-                engine.tensor_copy(
-                    out=dealt[:].rearrange("p (t b i) -> p b t i", t=PACK, i=16)[:, :, t : t + planes_a_copy, :],
-                    in_=scales[:].rearrange("p (b i t) -> p b t i", t=PACK, i=16)[:, :, t : t + planes_a_copy, :],
-                )
-            return dealt
+        def deal_weights(dealt, words, scales, planes):
+            deal(dealt[1], scales, 16, planes)
+            deal(dealt[0], words, 4, planes)
 
-        w1_dealt_words = deal_words("w1", w1w)
-        identity = sb("identity", [P, P], F32, tag="w1w_then_identity")
+        w1_dealt = (sb("w1_words", [P, PACK * P], I32), sb("w1_scales", [P, PACK * P], U8))
+        w2_dealt = (sb("w2_words", [P, PACK * P], I32), sb("w2_scales", [P, PACK * P], U8))
+        identity = sb("identity", [P, P], F32)
         make_identity(nc, identity[:])
 
         picked_scales = sb("picked_scales", [P, S], U8)
@@ -107,8 +102,9 @@ def tile_picked_minmod_none_po_kernel(
         first_half, second_half, all_columns = slice(0, HALF), slice(HALF, S), slice(0, S)
         nc.vector.tensor_copy(picked_scales[:], xs[:].indirect(offs_sb[:]))
         nc.vector.tensor_copy(picked_words[:, first_half], xw[:].indirect(entries(offs_sb, 0, HALF)))
-        w1_dealt = (w1_dealt_words, deal_scales("w1", w1s, nc.gpsimd, 1))
+        deal_weights(w1_dealt, w1w, w1s, slice(0, 1))
         nc.vector.tensor_copy(picked_words[:, second_half], xw[:].indirect(entries(offs_sb, HALF, HALF)))
+        deal_weights(w1_dealt, w1w, w1s, slice(1, PACK))
 
         def product(dst, weights, t, words, scales):
             cols = slice(P * t, P * (t + 1))
@@ -138,7 +134,7 @@ def tile_picked_minmod_none_po_kernel(
         first_layer(0, second_half, True)
         for t in range(1, PACK):
             first_layer(t, all_columns, False)
-        w2_dealt = (deal_words("w2", w2w), deal_scales("w2", w2s, nc.vector, PACK))
+        deal_weights(w2_dealt, w2w, w2s, slice(0, PACK))
 
         def add_transposed(dst, src, start, stop):
             nc.tensor.matmul(dst, src, identity[:], is_transpose=True, start=start, stop=stop)

@@ -65,8 +65,8 @@ def tile_picked_minmod_none_po_kernel(
         for scale_tile in (w1s, w2s):
             nc.gpsimd.memset(scale_tile[:].bitcast(I32), 0)
 
-        nc.sync.dma_start(out=xw[:, :X_AHEAD].bitcast(I32), in_=words_of(x_words)[:, :X_AHEAD])
         nc.sync.dma_start(offs_sb[:], offs)
+        nc.sync.dma_start(out=xw[:, :X_AHEAD].bitcast(I32), in_=words_of(x_words)[:, :X_AHEAD])
         load_scale_rows(xs, x_scales)
         nc.sync.dma_start(out=xw[:, X_AHEAD:].bitcast(I32), in_=words_of(x_words)[:, X_AHEAD:])
         nc.sync.dma_start(out=w1w[:], in_=words_of(w1_words))
@@ -82,15 +82,11 @@ def tile_picked_minmod_none_po_kernel(
         nc.scalar.activation(half_gain[:], gain[:], COPY, scale=0.5)
         nc.scalar.activation(minus_half_gain[:], gain[:], COPY, scale=-0.5)
 
-        def deal(dealt, source, run, planes):
-            nc.vector.tensor_copy(
+        def deal(engine, dealt, source, run, planes):
+            engine.tensor_copy(
                 out=dealt[:].rearrange("p (t b i) -> p b t i", t=PACK, i=run)[:, :, planes, :],
                 in_=source[:].rearrange("p (b i t) -> p b t i", t=PACK, i=run)[:, :, planes, :],
             )
-
-        def deal_weights(dealt, words, scales, planes):
-            deal(dealt[1], scales, 16, planes)
-            deal(dealt[0], words, 4, planes)
 
         w1_dealt = (sb("w1_words", [P, PACK * P], I32), sb("w1_scales", [P, PACK * P], U8))
         w2_dealt = (sb("w2_words", [P, PACK * P], I32), sb("w2_scales", [P, PACK * P], U8))
@@ -102,9 +98,11 @@ def tile_picked_minmod_none_po_kernel(
         first_half, second_half, all_columns = slice(0, HALF), slice(HALF, S), slice(0, S)
         nc.vector.tensor_copy(picked_scales[:], xs[:].indirect(offs_sb[:]))
         nc.vector.tensor_copy(picked_words[:, first_half], xw[:].indirect(entries(offs_sb, 0, HALF)))
-        deal_weights(w1_dealt, w1w, w1s, slice(0, 1))
+        deal(nc.vector, w1_dealt[0], w1w, 4, slice(0, 1))
+        for t in range(PACK):
+            deal(nc.gpsimd, w1_dealt[1], w1s, 16, slice(t, t + 1))
         nc.vector.tensor_copy(picked_words[:, second_half], xw[:].indirect(entries(offs_sb, HALF, HALF)))
-        deal_weights(w1_dealt, w1w, w1s, slice(1, PACK))
+        deal(nc.vector, w1_dealt[0], w1w, 4, slice(1, PACK))
 
         def product(dst, weights, t, words, scales):
             cols = slice(P * t, P * (t + 1))
@@ -134,7 +132,8 @@ def tile_picked_minmod_none_po_kernel(
         first_layer(0, second_half, True)
         for t in range(1, PACK):
             first_layer(t, all_columns, False)
-        deal_weights(w2_dealt, w2w, w2s, slice(0, PACK))
+        deal(nc.vector, w2_dealt[0], w2w, 4, slice(0, PACK))
+        deal(nc.vector, w2_dealt[1], w2s, 16, slice(0, PACK))
 
         def add_transposed(dst, src, start, stop):
             nc.tensor.matmul(dst, src, identity[:], is_transpose=True, start=start, stop=stop)
@@ -176,7 +175,7 @@ def tile_picked_minmod_none_po_kernel(
                 a_planes(c0)[:, t, in_half(c0, n)], minus[t][:].indirect(entries(west_sb, c0, n)), plus[t][:, c0 : c0 + n], ALU.add
             )
 
-        capped, limited, z_bf16, z_mx, out_bf16 = {}, {}, {}, {}, {}
+        capped, limited, z_bf16, z_mx, out_bf16, out_f32 = {}, {}, {}, {}, {}, {}
 
         def cap(c0):
             capped[c0] = sb("u%d" % c0, [P, PACK, PIECE], F32)
@@ -219,15 +218,12 @@ def tile_picked_minmod_none_po_kernel(
             zw, zs = z_mx[c0]
             result = sb("result%d" % c0, [P, PACK, PIECE], F32)
             rounded = sb("rounded%d" % c0, [P, PIECE, PACK], BF16)
-            if c0 == S - PIECE:
+            if c0 >= HALF:
                 for pair in range(0, PACK, 2):
                     acc = bank("acc", [P, 2, PIECE])
                     for t in range(2):
                         product(acc[:, t, :], w2_dealt, pair + t, zw[:], zs[:])
                     nc.scalar.copy(result[:, pair : pair + 2, :], acc[:])
-                nc.vector.tensor_copy(
-                    rounded[:].rearrange("p (c i) t -> p c t i", i=4), result[:].rearrange("p t (c i) -> p c t i", i=4)
-                )
             else:
                 acc = bank("acc", [P, PACK, PIECE])
                 for t in range(PACK):
@@ -236,6 +232,12 @@ def tile_picked_minmod_none_po_kernel(
                 nc.scalar.copy(result[:], acc[:])
             nc.sync.dma_start(out=out_rows[:, :, c0 : c0 + PIECE], in_=result[:])
             out_bf16[c0] = rounded
+            out_f32[c0] = result
+
+        def round_on_vector(c0):
+            nc.vector.tensor_copy(
+                out_bf16[c0][:].rearrange("p (c i) t -> p c t i", i=4), out_f32[c0][:].rearrange("p t (c i) -> p c t i", i=4)
+            )
 
         out_codes = sb("out_codes", [P, S], U32)
 
@@ -263,19 +265,26 @@ def tile_picked_minmod_none_po_kernel(
             second_layer(piece)
             for t in planes:
                 west_diff(t, piece2, PIECE)
-        for t, step in enumerate((cap, limit, edge_on_vector, quantise_z)):
-            west_diff(t, piece3, PIECE)
-            step(piece2)
-        second_layer(piece2)
+        west_diff(0, piece3, PIECE)
+        west_diff(1, piece3, PIECE)
+        cap(piece2)
+        west_diff(2, piece3, PIECE)
+        west_diff(3, piece3, PIECE)
+        limit(piece2)
         cap(piece3)
-        quantise_out(piece0)
+        edge_on_vector(piece2)
         limit(piece3)
-        quantise_out(piece1)
+        quantise_z(piece2)
+        second_layer(piece2)
         edge_on_vector(piece3)
+        quantise_out(piece0)
         quantise_z(piece3)
+        second_layer(piece3)
+        quantise_out(piece1)
+        round_on_vector(piece2)
         quantise_out(piece2)
         store_codes(slice(0, piece3))
-        second_layer(piece3)
+        round_on_vector(piece3)
         quantise_out(piece3)
         store_codes(slice(piece3, S))
         for q in range(QUADRANTS):

@@ -59,11 +59,10 @@ def tile_picked_minmod_none_po_kernel(
         w2w = sb("w2w", [P, N], I32)
         w2s = sb("w2s", [P, N], U8)
         gain = sb("gain", [P, PACK], F32)
-        w1s = sb("w1s", [P, H], U8)
+        w1s = sb("w1s", [P, H], U8, tag="w1s_then_words")
 
-        nc.vector.memset(xs[:].bitcast(I32), 0)
-        for scale_tile in (w1s, w2s):
-            nc.gpsimd.memset(scale_tile[:].bitcast(I32), 0)
+        for scale_tile in (xs, w1s, w2s):
+            nc.vector.memset(scale_tile[:].bitcast(I32), 0)
 
         nc.sync.dma_start(offs_sb[:], offs)
         nc.sync.dma_start(out=xw[:, :X_AHEAD].bitcast(I32), in_=words_of(x_words)[:, :X_AHEAD])
@@ -84,12 +83,14 @@ def tile_picked_minmod_none_po_kernel(
 
         def deal(engine, dealt, source, run, planes):
             engine.tensor_copy(
-                out=dealt[:].rearrange("p (t b i) -> p b t i", t=PACK, i=run)[:, :, planes, :],
+                out=dealt.rearrange("p (t b i) -> p b t i", t=planes.stop - planes.start, i=run),
                 in_=source[:].rearrange("p (b i t) -> p b t i", t=PACK, i=run)[:, :, planes, :],
             )
 
-        w1_dealt = (sb("w1_words", [P, PACK * P], I32), sb("w1_scales", [P, PACK * P], U8))
-        w2_dealt = (sb("w2_words", [P, PACK * P], I32), sb("w2_scales", [P, PACK * P], U8))
+        w1_first_words = sb("w1_first_words", [P, P], I32)
+        w1_scales_dealt = sb("w1_scales", [P, PACK * P], U8)
+        w2_words_dealt = sb("w2_words", [P, PACK * P], I32)
+        w2_scales_dealt = sb("w2_scales", [P, PACK * P], U8)
         identity = sb("identity", [P, P], F32)
         make_identity(nc, identity[:])
 
@@ -98,18 +99,24 @@ def tile_picked_minmod_none_po_kernel(
         first_half, second_half, all_columns = slice(0, HALF), slice(HALF, S), slice(0, S)
         nc.vector.tensor_copy(picked_scales[:], xs[:].indirect(offs_sb[:]))
         nc.vector.tensor_copy(picked_words[:, first_half], xw[:].indirect(entries(offs_sb, 0, HALF)))
-        deal(nc.vector, w1_dealt[0], w1w, 4, slice(0, 1))
-        for t in range(PACK):
-            deal(nc.gpsimd, w1_dealt[1], w1s, 16, slice(t, t + 1))
+        deal(nc.vector, w1_scales_dealt[:, :P], w1s, 16, slice(0, 1))
+        deal(nc.vector, w1_first_words[:], w1w, 4, slice(0, 1))
         nc.vector.tensor_copy(picked_words[:, second_half], xw[:].indirect(entries(offs_sb, HALF, HALF)))
-        deal(nc.vector, w1_dealt[0], w1w, 4, slice(1, PACK))
+        deal(nc.vector, w1_scales_dealt[:, P:], w1s, 16, slice(1, PACK))
+        w1_other_words = sb("w1_other_words", [P, (PACK - 1) * P], I32, tag="w1s_then_words")
+        deal(nc.vector, w1_other_words[:], w1w, 4, slice(1, PACK))
+
+        def plane(tile, t):
+            return tile[:, P * t : P * (t + 1)]
+
+        w1_dealt = [(plane(w1_other_words, t - 1) if t else w1_first_words[:], plane(w1_scales_dealt, t)) for t in range(PACK)]
+        w2_dealt = [(plane(w2_words_dealt, t), plane(w2_scales_dealt, t)) for t in range(PACK)]
 
         def product(dst, weights, t, words, scales):
-            cols = slice(P * t, P * (t + 1))
             nc.tensor.matmul_mx(
                 out=dst,
-                lhsT=weights[0][:, cols].bitcast(FP8X4),
-                lhsT_scale=weights[1][:, cols],
+                lhsT=weights[t][0].bitcast(FP8X4),
+                lhsT_scale=weights[t][1],
                 rhs=words.bitcast(FP8X4),
                 rhs_scale=scales,
                 start=True,
@@ -132,8 +139,8 @@ def tile_picked_minmod_none_po_kernel(
         first_layer(0, second_half, True)
         for t in range(1, PACK):
             first_layer(t, all_columns, False)
-        deal(nc.vector, w2_dealt[0], w2w, 4, slice(0, PACK))
-        deal(nc.vector, w2_dealt[1], w2s, 16, slice(0, PACK))
+        deal(nc.vector, w2_words_dealt[:], w2w, 4, slice(0, PACK))
+        deal(nc.vector, w2_scales_dealt[:], w2s, 16, slice(0, PACK))
 
         def add_transposed(dst, src, start, stop):
             nc.tensor.matmul(dst, src, identity[:], is_transpose=True, start=start, stop=stop)

@@ -23,6 +23,7 @@ GROUP = 16
 HALF = S // 2
 PIECE = 128
 PSUM_BANKS = 8
+LINE_BYTES = 16
 X_AHEAD = 3 * T // 8
 
 
@@ -59,7 +60,7 @@ def tile_picked_minmod_none_po_kernel(
         w2w = sb("w2w", [P, N], I32)
         w2s = sb("w2s", [P, N], U8)
         gain = sb("gain", [P, PACK], F32)
-        w1s = sb("w1s", [P, H], U8, tag="w1s_then_words")
+        w1s = sb("w1s", [P, H], U8, tag="w1s_then_w1_words")
 
         for scale_tile in (xs, w1s, w2s):
             nc.vector.memset(scale_tile[:].bitcast(I32), 0)
@@ -77,12 +78,16 @@ def tile_picked_minmod_none_po_kernel(
         load_scale_rows(w2s, w2_scales)
 
         half_gain = sb("half_gain", [P, PACK], F32)
-        minus_half_gain = sb("minus_half_gain", [P, PACK], F32)
+        b_rows = sb("b_rows", [P, PACK + 1, HALF], F32)
+        minus_half_gain = b_rows[:, 0, :PACK]
         nc.scalar.activation(half_gain[:], gain[:], COPY, scale=0.5)
-        nc.scalar.activation(minus_half_gain[:], gain[:], COPY, scale=-0.5)
+        nc.scalar.activation(minus_half_gain, gain[:], COPY, scale=-0.5)
 
-        def deal(engine, dealt, source, run, planes):
-            engine.tensor_copy(
+        first_plane, other_planes, all_planes = slice(0, 1), slice(1, PACK), slice(0, PACK)
+        words_a_line, scales_a_line = LINE_BYTES // 4, LINE_BYTES
+
+        def deal(dealt, source, run, planes):
+            nc.vector.tensor_copy(
                 out=dealt.rearrange("p (t b i) -> p b t i", t=planes.stop - planes.start, i=run),
                 in_=source[:].rearrange("p (b i t) -> p b t i", t=PACK, i=run)[:, :, planes, :],
             )
@@ -99,12 +104,12 @@ def tile_picked_minmod_none_po_kernel(
         first_half, second_half, all_columns = slice(0, HALF), slice(HALF, S), slice(0, S)
         nc.vector.tensor_copy(picked_scales[:], xs[:].indirect(offs_sb[:]))
         nc.vector.tensor_copy(picked_words[:, first_half], xw[:].indirect(entries(offs_sb, 0, HALF)))
-        deal(nc.vector, w1_scales_dealt[:, :P], w1s, 16, slice(0, 1))
-        deal(nc.vector, w1_first_words[:], w1w, 4, slice(0, 1))
+        deal(w1_scales_dealt[:, :P], w1s, scales_a_line, first_plane)
+        deal(w1_first_words[:], w1w, words_a_line, first_plane)
         nc.vector.tensor_copy(picked_words[:, second_half], xw[:].indirect(entries(offs_sb, HALF, HALF)))
-        deal(nc.vector, w1_scales_dealt[:, P:], w1s, 16, slice(1, PACK))
-        w1_other_words = sb("w1_other_words", [P, (PACK - 1) * P], I32, tag="w1s_then_words")
-        deal(nc.vector, w1_other_words[:], w1w, 4, slice(1, PACK))
+        deal(w1_scales_dealt[:, P:], w1s, scales_a_line, other_planes)
+        w1_other_words = sb("w1_other_words", [P, (PACK - 1) * P], I32, tag="w1s_then_w1_words")
+        deal(w1_other_words[:], w1w, words_a_line, other_planes)
 
         def plane(tile, t):
             return tile[:, P * t : P * (t + 1)]
@@ -139,8 +144,8 @@ def tile_picked_minmod_none_po_kernel(
         first_layer(0, second_half, True)
         for t in range(1, PACK):
             first_layer(t, all_columns, False)
-        deal(nc.vector, w2_words_dealt[:], w2w, 4, slice(0, PACK))
-        deal(nc.vector, w2_scales_dealt[:], w2s, 16, slice(0, PACK))
+        deal(w2_words_dealt[:], w2w, words_a_line, all_planes)
+        deal(w2_scales_dealt[:], w2s, scales_a_line, all_planes)
 
         def add_transposed(dst, src, start, stop):
             nc.tensor.matmul(dst, src, identity[:], is_transpose=True, start=start, stop=stop)
@@ -156,7 +161,6 @@ def tile_picked_minmod_none_po_kernel(
         for t in range(PACK):
             nc.scalar.activation(centre[:, t, :], plus[t][:, second_half], COPY, scale=2.0)
 
-        b_rows = sb("b_rows", [P, PACK + 1, HALF], F32)
         a_half = {}
 
         def b_planes(c0):

@@ -15,6 +15,7 @@ U8 = mybir.dt.uint8
 FP8X4 = mybir.dt.float8_e4m3fn_x4
 ALU = mybir.AluOpType
 COPY = mybir.ActivationFunctionType.Copy
+RELU = mybir.ActivationFunctionType.Relu
 
 P = 128
 PACK = 4
@@ -22,7 +23,6 @@ QUADRANTS = 4
 GROUP = 16
 HALF = S // 2
 PIECE = 128
-PSUM_BANKS = 8
 LINE_BYTES = 16
 X_AHEAD = 3 * T // 8
 
@@ -33,13 +33,13 @@ def tile_picked_minmod_none_po_kernel(
     nc = tc.nc
     with ExitStack() as ctx:
         keep = ctx.enter_context(tc.tile_pool(name="keep", bufs=1))
-        psum = ctx.enter_context(tc.psum_pool(name="psum", bufs=PSUM_BANKS))
+        psum = ctx.enter_context(tc.psum_pool(name="psum", bufs=1))
 
         def sb(name, shape, dtype, tag=""):
             return keep.tile(shape, dtype, name=name, tag=tag, align_bytes=64)
 
-        def bank(name, shape):
-            return psum.tile(shape, F32, name=name, tag="bank")
+        def bank(name, shape, number):
+            return psum.tile(shape, F32, name=name, tag="bank%d" % number)
 
         def words_of(dram):
             return dram[0].rearrange("p n t -> p (n t)").bitcast(I32)
@@ -94,8 +94,6 @@ def tile_picked_minmod_none_po_kernel(
 
         w1_first_words = sb("w1_first_words", [P, P], I32)
         w1_scales_dealt = sb("w1_scales", [P, PACK * P], U8)
-        w2_words_dealt = sb("w2_words", [P, PACK * P], I32)
-        w2_scales_dealt = sb("w2_scales", [P, PACK * P], U8)
         identity = sb("identity", [P, P], F32)
         make_identity(nc, identity[:])
 
@@ -115,7 +113,6 @@ def tile_picked_minmod_none_po_kernel(
             return tile[:, P * t : P * (t + 1)]
 
         w1_dealt = [(plane(w1_other_words, t - 1) if t else w1_first_words[:], plane(w1_scales_dealt, t)) for t in range(PACK)]
-        w2_dealt = [(plane(w2_words_dealt, t), plane(w2_scales_dealt, t)) for t in range(PACK)]
 
         def product(dst, weights, t, words, scales):
             nc.tensor.matmul_mx(
@@ -131,8 +128,8 @@ def tile_picked_minmod_none_po_kernel(
         plus = [sb("plus%d" % t, [P, S], F32) for t in range(PACK)]
         minus = [sb("minus%d" % t, [P, S], F32) for t in range(PACK)]
 
-        def first_layer(t, cols, plus_on_vector):
-            y = bank("y", [P, cols.stop - cols.start])
+        def first_layer(t, cols, plus_on_vector, number):
+            y = bank("y", [P, cols.stop - cols.start], number)
             product(y[:], w1_dealt, t, picked_words[:, cols], picked_scales[:, cols])
             if plus_on_vector:
                 nc.vector.tensor_scalar(plus[t][:, cols], y[:], half_gain[:, t : t + 1], None, ALU.mult)
@@ -140,38 +137,37 @@ def tile_picked_minmod_none_po_kernel(
                 nc.scalar.activation(plus[t][:, cols], y[:], COPY, scale=half_gain[:, t : t + 1])
             nc.scalar.activation(minus[t][:, cols], y[:], COPY, scale=minus_half_gain[:, t : t + 1])
 
-        first_layer(0, first_half, False)
-        first_layer(0, second_half, True)
+        first_layer(0, first_half, False, 0)
+        first_layer(0, second_half, True, 1)
         for t in range(1, PACK):
-            first_layer(t, all_columns, False)
-        deal(w2_words_dealt[:], w2w, words_a_line, all_planes)
-        deal(w2_scales_dealt[:], w2s, scales_a_line, all_planes)
+            first_layer(t, all_columns, False, t + 1)
 
         def add_transposed(dst, src, start, stop):
             nc.tensor.matmul(dst, src, identity[:], is_transpose=True, start=start, stop=stop)
 
         turned = {}
         for c0 in range(0, HALF, PIECE):
-            turned[c0] = bank("turned", [P, PACK, P])
+            turned[c0] = bank("turned", [P, PACK, P], 5 + c0 // PIECE)
             for t in range(PACK):
                 add_transposed(turned[c0][:, t, :], plus[t][:, c0 : c0 + PIECE], t == 0, False)
                 add_transposed(turned[c0][:, t, :], plus[t][:, c0 : c0 + PIECE], False, False)
 
-        centre = sb("centre", [P, PACK, HALF], F32)
-        for t in range(PACK):
-            nc.scalar.activation(centre[:, t, :], plus[t][:, second_half], COPY, scale=2.0)
-
-        a_half = {}
+        a_tiles = {}
 
         def b_planes(c0):
             first_row = 1 if c0 < HALF else 0
             return b_rows[:, first_row : first_row + PACK, :]
 
         def a_planes(c0):
+            if c0 == S - PIECE:
+                return late_steps[0][:, 0]
             h0 = c0 - c0 % HALF
-            if h0 not in a_half:
-                a_half[h0] = sb("a%d" % h0, [P, PACK, HALF], F32, tag="a")
-            return a_half[h0]
+            if h0 not in a_tiles:
+                a_tiles[h0] = sb("a%d" % h0, [P, PACK, PIECE if h0 else HALF], F32, tag="a")
+            return a_tiles[h0]
+
+        def in_a(c0, n):
+            return slice(c0, c0 + n) if c0 < HALF else slice(0, n)
 
         def in_half(c0, n):
             return slice(c0 % HALF, c0 % HALF + n)
@@ -183,43 +179,72 @@ def tile_picked_minmod_none_po_kernel(
 
         def west_diff(t, c0, n):
             nc.vector.tensor_tensor(
-                a_planes(c0)[:, t, in_half(c0, n)], minus[t][:].indirect(entries(west_sb, c0, n)), plus[t][:, c0 : c0 + n], ALU.add
+                a_planes(c0)[:, t, in_a(c0, n)], minus[t][:].indirect(entries(west_sb, c0, n)), plus[t][:, c0 : c0 + n], ALU.add
             )
 
         capped, limited, z_bf16, z_mx, out_bf16, out_f32 = {}, {}, {}, {}, {}, {}
 
+        z_early = sb("z_early", [P, HALF * PACK], BF16)
+        late_steps, centre = [], {}
+
         def cap(c0):
-            capped[c0] = sb("u%d" % c0, [P, PACK, PIECE], F32)
+            capped[c0] = late_steps[0][:, 1] if c0 == HALF else sb("u%d" % c0, [P, PACK, PIECE], F32)
             cols = in_half(c0, PIECE)
-            nc.vector.scalar_tensor_tensor(capped[c0][:], a_planes(c0)[:, :, cols], 0.0, b_planes(c0)[:, :, cols], ALU.max, ALU.min)
+            nc.vector.scalar_tensor_tensor(capped[c0][:], a_planes(c0)[:, :, in_a(c0, PIECE)], 0.0, b_planes(c0)[:, :, cols], ALU.max, ALU.min)
 
         def limit(c0):
             limited[c0] = sb("m%d" % c0, [P, PACK, PIECE], F32)
-            nc.vector.scalar_tensor_tensor(limited[c0][:], a_planes(c0)[:, :, in_half(c0, PIECE)], 0.0, capped[c0][:], ALU.min, ALU.max)
+            nc.vector.scalar_tensor_tensor(limited[c0][:], a_planes(c0)[:, :, in_a(c0, PIECE)], 0.0, capped[c0][:], ALU.min, ALU.max)
 
         def edge_on_vector(c0):
             z_bf16[c0] = sb("z%d" % c0, [P, PIECE * PACK], BF16)
             nc.vector.tensor_tensor(
                 z_bf16[c0][:].rearrange("p (c i t) -> p c t i", t=PACK, i=2),
                 limited[c0][:].rearrange("p t (c i) -> p c t i", i=2),
-                centre[:, :, in_half(c0, PIECE)].rearrange("p t (c i) -> p c t i", i=2),
+                centre[c0].rearrange("p t (c i) -> p c t i", i=2),
                 ALU.add,
             )
 
-        def edge_on_tensor(c0):
+        lifted = {}
+
+        total = {0: bank("total", [P, PACK, P], 7), PIECE: bank("total", [P, PACK, P], 0)}
+
+        def turn_b(t):
+            for c0 in total:
+                add_transposed(total[c0][:, t, :], b_planes(c0)[:, t, in_half(c0, PIECE)], t == 0, False)
+
+        def turn_below(planes):
+            below = sb("below", [P, planes.stop - planes.start, HALF], F32, tag="below%d_then_w2" % planes.start)
+            nc.scalar.activation(below[:], a_planes(0)[:, planes, :], RELU, scale=-1.0)
+            for c0 in total:
+                for t in range(planes.start, planes.stop):
+                    add_transposed(total[c0][:, t, :], below[:, t - planes.start, in_half(c0, PIECE)], False, t == PACK - 1)
+
+        def lift(c0):
+            lifted[c0] = sb("lifted%d" % c0, [P, PACK, P], F32)
+            nc.scalar.activation(lifted[c0][:], total[c0][:], RELU, scale=-1.0)
+
+        def edge_without_limit(c0, number):
             for t in range(PACK):
-                add_transposed(turned[c0][:, t, :], limited[c0][:, t, :], False, t == PACK - 1)
-            pairs = sb("pairs%d" % c0, [P, 2, P, 2], BF16)
-            nc.scalar.copy(pairs[:], turned[c0][:].rearrange("j (u e) p -> j u p e", e=2))
-            back = bank("back", [P, 2, P])
-            for u in range(2):
-                nc.tensor.transpose(back[:, u, :], pairs[:, u, :, :].rearrange("j p e -> j (p e)").bitcast(F32), identity[:])
-            z_bf16[c0] = sb("z%d" % c0, [P, PIECE * PACK], BF16)
-            nc.scalar.copy(z_bf16[c0][:].bitcast(F32).rearrange("p (j u) -> p j u", u=2), back[:].rearrange("p u j -> p j u"))
+                add_transposed(turned[c0][:, t, :], capped[c0][:, t, :], False, t == PACK - 1)
+            summed = sb("summed%d" % c0, [P, PACK, P], F32, tag="summed_then_centre" if c0 else "")
+            nc.scalar.copy(summed[:], turned[c0][:])
+            whole = bank("whole", [P, PACK, P], number)
+            for t in range(PACK):
+                add_transposed(whole[:, t, :], lifted[c0][:, t, :], t == 0, False)
+            for t in range(PACK):
+                add_transposed(whole[:, t, :], summed[:, t, :], False, t == PACK - 1)
+            nc.scalar.copy(z_early[:, c0 * PACK : (c0 + PIECE) * PACK].rearrange("p (j t) -> p j t", t=PACK), whole[:].rearrange("p t j -> p j t"))
 
         def quantise_z(c0):
             z_mx[c0] = (sb("zw%d" % c0, [P, PIECE], U32), sb("zs%d" % c0, [P, PIECE], U8))
             nc.vector.quantize_mx(out=z_mx[c0][0][:].bitcast(FP8X4), scales=z_mx[c0][1][:], in_=z_bf16[c0][:])
+
+        def quantise_early_z():
+            words, scales = sb("zw_early", [P, HALF], U32), sb("zs_early", [P, HALF], U8)
+            nc.vector.quantize_mx(out=words[:].bitcast(FP8X4), scales=scales[:], in_=z_early[:])
+            for c0 in range(0, HALF, PIECE):
+                z_mx[c0] = (words[:, c0 : c0 + PIECE], scales[:, c0 : c0 + PIECE])
 
         out_rows = out_0.rearrange("(p t) j -> p t j", t=PACK)
         out_words = out_1[0].rearrange("p n t -> p (n t)").bitcast(I32)
@@ -231,12 +256,12 @@ def tile_picked_minmod_none_po_kernel(
             rounded = sb("rounded%d" % c0, [P, PIECE, PACK], BF16)
             if c0 >= HALF:
                 for pair in range(0, PACK, 2):
-                    acc = bank("acc", [P, 2, PIECE])
+                    acc = bank("acc", [P, 2, PIECE], (2 * (c0 // PIECE) + pair // 2 + 1) % 8)
                     for t in range(2):
                         product(acc[:, t, :], w2_dealt, pair + t, zw[:], zs[:])
                     nc.scalar.copy(result[:, pair : pair + 2, :], acc[:])
             else:
-                acc = bank("acc", [P, PACK, PIECE])
+                acc = bank("acc", [P, PACK, PIECE], 3 + c0 // PIECE)
                 for t in range(PACK):
                     product(acc[:, t, :], w2_dealt, t, zw[:], zs[:])
                 nc.scalar.copy(rounded[:], acc[:].rearrange("p t n -> p n t"))
@@ -265,22 +290,37 @@ def tile_picked_minmod_none_po_kernel(
         piece0, piece1, piece2, piece3 = range(0, S, PIECE)
         for t in range(PACK):
             east_diff(t, 0, HALF)
+            turn_b(t)
             west_diff(t, 0, HALF)
-        for step in (cap, limit, edge_on_tensor):
-            step(piece0)
-            step(piece1)
+            if t >= 2:
+                turn_below(slice(0, 3) if t == 2 else slice(3, 4))
+        w2_words_dealt = sb("w2_words", [P, PACK * P], I32, tag="below0_then_w2")
+        w2_scales_dealt = sb("w2_scales", [P, PACK * P], U8, tag="below3_then_w2")
+        w2_dealt = [(plane(w2_words_dealt, t), plane(w2_scales_dealt, t)) for t in range(PACK)]
+        lift(piece0)
+        lift(piece1)
+        cap(piece0)
+        cap(piece1)
+        deal(w2_words_dealt[:], w2w, words_a_line, all_planes)
+        deal(w2_scales_dealt[:], w2s, scales_a_line, all_planes)
+        edge_without_limit(piece0, 1)
+        edge_without_limit(piece1, 2)
+        late_steps.append(sb("late_steps", [P, 4, PACK, PIECE], F32, tag="summed_then_centre"))
+        for c0 in (piece2, piece3):
+            centre[c0] = late_steps[0][:, c0 // PIECE]
+        for t in range(PACK):
+            nc.scalar.activation(late_steps[0][:, 2:, t, :], plus[t][:, second_half].rearrange("p (k c) -> p k c", k=2), COPY, scale=2.0)
+
         for t in range(PACK):
             east_diff(t, HALF, HALF)
-        for piece, planes in ((piece0, (0, 1)), (piece1, (2, 3))):
-            quantise_z(piece)
-            second_layer(piece)
-            for t in planes:
-                west_diff(t, piece2, PIECE)
-        west_diff(0, piece3, PIECE)
-        west_diff(1, piece3, PIECE)
+        for t in range(PACK):
+            west_diff(t, piece2, PIECE)
+        for t in range(PACK):
+            west_diff(t, piece3, PIECE)
         cap(piece2)
-        west_diff(2, piece3, PIECE)
-        west_diff(3, piece3, PIECE)
+        quantise_early_z()
+        second_layer(piece0)
+        second_layer(piece1)
         limit(piece2)
         cap(piece3)
         edge_on_vector(piece2)

@@ -45,8 +45,8 @@ def tile_picked_minmod_none_po_kernel(
             return dram[0].rearrange("p n t -> p (n t)").bitcast(I32)
 
         def load_scale_rows(tile, dram):
-            for q in range(QUADRANTS):
-                nc.sync.dma_start(out=tile[32 * q : 32 * q + 4, :].bitcast(I32), in_=dram[0, 4 * q : 4 * q + 4, :].bitcast(I32))
+            for r in range(4):
+                nc.sync.dma_start(out=tile[r:P:32, :].bitcast(I32), in_=dram[0, r:16:4, :].bitcast(I32))
 
         def entries(list_tile, c0, n):
             return list_tile[:, c0 // GROUP : (c0 + n) // GROUP]
@@ -72,9 +72,9 @@ def tile_picked_minmod_none_po_kernel(
         nc.sync.dma_start(out=w1w[:], in_=words_of(w1_words))
         load_scale_rows(w1s, w1_scales)
         nc.sync.dma_start(out=gain[:], in_=gn.rearrange("(p t) o -> p (t o)", t=PACK))
-        nc.sync.dma_start(out=w2w[:], in_=words_of(w2_words))
         nc.sync.dma_start(east_sb[:], east)
         nc.sync.dma_start(west_sb[:], west)
+        nc.sync.dma_start(out=w2w[:], in_=words_of(w2_words))
         load_scale_rows(w2s, w2_scales)
 
         half_gain = sb("half_gain", [P, PACK], F32)

@@ -72,9 +72,9 @@ def tile_picked_minmod_none_po_kernel(
         nc.sync.dma_start(out=w1w[:], in_=words_of(w1_words))
         load_scale_rows(w1s, w1_scales)
         nc.sync.dma_start(out=gain[:], in_=gn.rearrange("(p t) o -> p (t o)", t=PACK))
+        nc.sync.dma_start(out=w2w[:], in_=words_of(w2_words))
         nc.sync.dma_start(east_sb[:], east)
         nc.sync.dma_start(west_sb[:], west)
-        nc.sync.dma_start(out=w2w[:], in_=words_of(w2_words))
         load_scale_rows(w2s, w2_scales)
 
         half_gain = sb("half_gain", [P, PACK], F32)
@@ -125,7 +125,7 @@ def tile_picked_minmod_none_po_kernel(
                 stop=True,
             )
 
-        plus = [sb("plus%d" % t, [P, S], F32) for t in range(PACK)]
+        plus = [sb("plus%d" % t, [P, S], F32, tag="plus%d_then_cap" % t) for t in range(PACK)]
         minus = [sb("minus%d" % t, [P, S], F32) for t in range(PACK)]
 
         def first_layer(t, cols, plus_on_vector, number):
@@ -138,9 +138,12 @@ def tile_picked_minmod_none_po_kernel(
             nc.scalar.activation(minus[t][:, cols], y[:], COPY, scale=minus_half_gain[:, t : t + 1])
 
         first_layer(0, first_half, False, 0)
-        first_layer(0, second_half, True, 1)
+        first_layer(0, second_half, False, 1)
         for t in range(1, PACK):
             first_layer(t, all_columns, False, t + 1)
+
+        w2_words_dealt = sb("w2_words", [P, PACK * P], I32)
+        deal(w2_words_dealt[:], w2w, words_a_line, all_planes)
 
         def add_transposed(dst, src, start, stop):
             nc.tensor.matmul(dst, src, identity[:], is_transpose=True, start=start, stop=stop)
@@ -159,15 +162,13 @@ def tile_picked_minmod_none_po_kernel(
             return b_rows[:, first_row : first_row + PACK, :]
 
         def a_planes(c0):
-            if c0 == S - PIECE:
-                return late_steps[0][:, 0]
             h0 = c0 - c0 % HALF
             if h0 not in a_tiles:
-                a_tiles[h0] = sb("a%d" % h0, [P, PACK, PIECE if h0 else HALF], F32, tag="a")
+                a_tiles[h0] = sb("a%d" % h0, [P, PACK, HALF], F32, tag="a")
             return a_tiles[h0]
 
         def in_a(c0, n):
-            return slice(c0, c0 + n) if c0 < HALF else slice(0, n)
+            return in_half(c0, n)
 
         def in_half(c0, n):
             return slice(c0 % HALF, c0 % HALF + n)
@@ -188,12 +189,12 @@ def tile_picked_minmod_none_po_kernel(
         late_steps, centre = [], {}
 
         def cap(c0):
-            capped[c0] = late_steps[0][:, 1] if c0 == HALF else sb("u%d" % c0, [P, PACK, PIECE], F32)
+            capped[c0] = sb("u%d" % c0, [P, PACK, PIECE], F32, tag="plus1_then_cap" if c0 == S - PIECE else "")
             cols = in_half(c0, PIECE)
             nc.vector.scalar_tensor_tensor(capped[c0][:], a_planes(c0)[:, :, in_a(c0, PIECE)], 0.0, b_planes(c0)[:, :, cols], ALU.max, ALU.min)
 
         def limit(c0):
-            limited[c0] = sb("m%d" % c0, [P, PACK, PIECE], F32)
+            limited[c0] = sb("m%d" % c0, [P, PACK, PIECE], F32, tag="plus0_then_cap" if c0 == HALF else "")
             nc.vector.scalar_tensor_tensor(limited[c0][:], a_planes(c0)[:, :, in_a(c0, PIECE)], 0.0, capped[c0][:], ALU.min, ALU.max)
 
         def edge_on_vector(c0):
@@ -294,29 +295,27 @@ def tile_picked_minmod_none_po_kernel(
             west_diff(t, 0, HALF)
             if t >= 2:
                 turn_below(slice(0, 3) if t == 2 else slice(3, 4))
-        w2_words_dealt = sb("w2_words", [P, PACK * P], I32, tag="below0_then_w2")
         w2_scales_dealt = sb("w2_scales", [P, PACK * P], U8, tag="below3_then_w2")
         w2_dealt = [(plane(w2_words_dealt, t), plane(w2_scales_dealt, t)) for t in range(PACK)]
         lift(piece0)
         lift(piece1)
         cap(piece0)
         cap(piece1)
-        deal(w2_words_dealt[:], w2w, words_a_line, all_planes)
         deal(w2_scales_dealt[:], w2s, scales_a_line, all_planes)
         edge_without_limit(piece0, 1)
         edge_without_limit(piece1, 2)
-        late_steps.append(sb("late_steps", [P, 4, PACK, PIECE], F32, tag="summed_then_centre"))
+        late_steps.append(sb("late_steps", [P, 2, PACK, PIECE], F32, tag="summed_then_centre"))
         for c0 in (piece2, piece3):
-            centre[c0] = late_steps[0][:, c0 // PIECE]
+            centre[c0] = late_steps[0][:, c0 // PIECE - 2]
         for t in range(PACK):
-            nc.scalar.activation(late_steps[0][:, 2:, t, :], plus[t][:, second_half].rearrange("p (k c) -> p k c", k=2), COPY, scale=2.0)
+            nc.scalar.activation(late_steps[0][:, :, t, :], plus[t][:, second_half].rearrange("p (k c) -> p k c", k=2), COPY, scale=2.0)
 
         for t in range(PACK):
             east_diff(t, HALF, HALF)
-        for t in range(PACK):
-            west_diff(t, piece2, PIECE)
-        for t in range(PACK):
-            west_diff(t, piece3, PIECE)
+        for t in range(PACK - 1):
+            west_diff(t, HALF, HALF)
+        west_diff(PACK - 1, piece2, PIECE)
+        west_diff(PACK - 1, piece3, PIECE)
         cap(piece2)
         quantise_early_z()
         second_layer(piece0)

@@ -25,6 +25,7 @@ HALF = S // 2
 PIECE = 128
 LINE_BYTES = 16
 X_AHEAD = 3 * T // 8
+B_SHIFT = HALF + PIECE
 
 
 def tile_picked_minmod_none_po_kernel(
@@ -78,8 +79,8 @@ def tile_picked_minmod_none_po_kernel(
         load_scale_rows(w2s, w2_scales)
 
         half_gain = sb("half_gain", [P, PACK], F32)
-        b_rows = sb("b_rows", [P, PACK + 1, HALF], F32)
-        minus_half_gain = b_rows[:, 0, :PACK]
+        b_rows = sb("b_rows", [P, B_SHIFT + PACK * HALF], F32)
+        minus_half_gain = b_rows[:, :PACK]
         nc.scalar.activation(half_gain[:], gain[:], COPY, scale=0.5)
         nc.scalar.activation(minus_half_gain, gain[:], COPY, scale=-0.5)
 
@@ -135,7 +136,11 @@ def tile_picked_minmod_none_po_kernel(
                 nc.vector.tensor_scalar(plus[t][:, cols], y[:], half_gain[:, t : t + 1], None, ALU.mult)
             else:
                 nc.scalar.activation(plus[t][:, cols], y[:], COPY, scale=half_gain[:, t : t + 1])
-            nc.scalar.activation(minus[t][:, cols], y[:], COPY, scale=minus_half_gain[:, t : t + 1])
+            if t == PACK - 1:
+                for half in (first_half, second_half):
+                    nc.scalar.activation(minus[t][:, half], y[:, half], COPY, scale=minus_half_gain[:, t : t + 1])
+            else:
+                nc.scalar.activation(minus[t][:, cols], y[:], COPY, scale=minus_half_gain[:, t : t + 1])
 
         first_layer(0, first_half, False, 0)
         first_layer(0, second_half, False, 1)
@@ -158,8 +163,8 @@ def tile_picked_minmod_none_po_kernel(
         a_tiles = {}
 
         def b_planes(c0):
-            first_row = 1 if c0 < HALF else 0
-            return b_rows[:, first_row : first_row + PACK, :]
+            start = B_SHIFT if c0 < HALF else 0
+            return b_rows[:, start : start + PACK * HALF].rearrange("p (t c) -> p t c", t=PACK)
 
         def a_planes(c0):
             h0 = c0 - c0 % HALF
@@ -295,7 +300,7 @@ def tile_picked_minmod_none_po_kernel(
             west_diff(t, 0, HALF)
             if t >= 2:
                 turn_below(slice(0, 3) if t == 2 else slice(3, 4))
-        w2_scales_dealt = sb("w2_scales", [P, PACK * P], U8, tag="below3_then_w2")
+        w2_scales_dealt = sb("w2_scales", [P, PACK * P], U8)
         w2_dealt = [(plane(w2_words_dealt, t), plane(w2_scales_dealt, t)) for t in range(PACK)]
         lift(piece0)
         lift(piece1)

@@ -102,10 +102,9 @@ def tile_picked_minmod_none_po_kernel(
         picked_words = sb("picked_words", [P, S], U32)
         first_half, second_half, all_columns = slice(0, HALF), slice(HALF, S), slice(0, S)
         nc.vector.tensor_copy(picked_scales[:], xs[:].indirect(offs_sb[:]))
-        nc.vector.tensor_copy(picked_words[:, first_half], xw[:].indirect(entries(offs_sb, 0, HALF)))
+        nc.vector.tensor_copy(picked_words[:], xw[:].indirect(offs_sb[:]))
         deal(w1_scales_dealt[:, :P], w1s, scales_a_line, first_plane)
         deal(w1_first_words[:], w1w, words_a_line, first_plane)
-        nc.vector.tensor_copy(picked_words[:, second_half], xw[:].indirect(entries(offs_sb, HALF, HALF)))
         deal(w1_scales_dealt[:, P:], w1s, scales_a_line, other_planes)
         w1_other_words = sb("w1_other_words", [P, (PACK - 1) * P], I32, tag="w1s_then_w1_words")
         deal(w1_other_words[:], w1w, words_a_line, other_planes)
@@ -126,7 +125,7 @@ def tile_picked_minmod_none_po_kernel(
                 stop=True,
             )
 
-        plus = [sb("plus%d" % t, [P, S], F32, tag="plus%d_then_cap" % t) for t in range(PACK)]
+        plus = [sb("plus%d" % t, [P, S], F32, tag="" if t else "plus0_then_late_steps") for t in range(PACK)]
         minus = [sb("minus%d" % t, [P, S], F32) for t in range(PACK)]
 
         def first_layer(t, cols, plus_on_vector, number):
@@ -191,22 +190,29 @@ def tile_picked_minmod_none_po_kernel(
         capped, limited, z_bf16, z_mx, out_bf16, out_f32 = {}, {}, {}, {}, {}, {}
 
         z_early = sb("z_early", [P, HALF * PACK], BF16)
-        late_steps, centre = [], {}
+        centre = {}
+        shared = sb("shared", [P, 3 * PACK, PIECE], F32)
+        held = {}
 
         def cap(c0):
-            capped[c0] = sb("u%d" % c0, [P, PACK, PIECE], F32, tag="plus1_then_cap" if c0 == S - PIECE else "")
+            if c0 < HALF:
+                capped[c0] = shared[:, PACK * (1 + c0 // PIECE) : PACK * (2 + c0 // PIECE), :]
+            elif c0 == HALF:
+                capped[c0] = sb("u%d" % c0, [P, PACK, PIECE], F32)[:]
+            else:
+                capped[c0] = held[0][:, 1]
             cols = in_half(c0, PIECE)
-            nc.vector.scalar_tensor_tensor(capped[c0][:], a_planes(c0)[:, :, in_a(c0, PIECE)], 0.0, b_planes(c0)[:, :, cols], ALU.max, ALU.min)
+            nc.vector.scalar_tensor_tensor(capped[c0], a_planes(c0)[:, :, in_a(c0, PIECE)], 0.0, b_planes(c0)[:, :, cols], ALU.max, ALU.min)
 
         def limit(c0):
-            limited[c0] = sb("m%d" % c0, [P, PACK, PIECE], F32, tag="plus0_then_cap" if c0 == HALF else "")
-            nc.vector.scalar_tensor_tensor(limited[c0][:], a_planes(c0)[:, :, in_a(c0, PIECE)], 0.0, capped[c0][:], ALU.min, ALU.max)
+            limited[c0] = held[0][:, 0] if c0 == HALF else sb("m%d" % c0, [P, PACK, PIECE], F32)[:]
+            nc.vector.scalar_tensor_tensor(limited[c0], a_planes(c0)[:, :, in_a(c0, PIECE)], 0.0, capped[c0], ALU.min, ALU.max)
 
         def edge_on_vector(c0):
             z_bf16[c0] = sb("z%d" % c0, [P, PIECE * PACK], BF16)
             nc.vector.tensor_tensor(
                 z_bf16[c0][:].rearrange("p (c i t) -> p c t i", t=PACK, i=2),
-                limited[c0][:].rearrange("p t (c i) -> p c t i", i=2),
+                limited[c0].rearrange("p t (c i) -> p c t i", i=2),
                 centre[c0].rearrange("p t (c i) -> p c t i", i=2),
                 ALU.add,
             )
@@ -233,8 +239,8 @@ def tile_picked_minmod_none_po_kernel(
         def edge_without_limit(c0, number):
             for t in range(PACK):
                 add_transposed(turned[c0][:, t, :], capped[c0][:, t, :], False, t == PACK - 1)
-            summed = sb("summed%d" % c0, [P, PACK, P], F32, tag="summed_then_centre" if c0 else "")
-            nc.scalar.copy(summed[:], turned[c0][:])
+            summed = shared[:, :PACK, :] if c0 else sb("summed0", [P, PACK, P], F32)[:]
+            nc.scalar.copy(summed, turned[c0][:])
             whole = bank("whole", [P, PACK, P], number)
             for t in range(PACK):
                 add_transposed(whole[:, t, :], lifted[c0][:, t, :], t == 0, False)
@@ -309,11 +315,11 @@ def tile_picked_minmod_none_po_kernel(
         deal(w2_scales_dealt[:], w2s, scales_a_line, all_planes)
         edge_without_limit(piece0, 1)
         edge_without_limit(piece1, 2)
-        late_steps.append(sb("late_steps", [P, 2, PACK, PIECE], F32, tag="summed_then_centre"))
+        both_centres = shared[:, 2 : 2 + 2 * PACK, :].rearrange("p (t k) c -> p k t c", k=2)
         for c0 in (piece2, piece3):
-            centre[c0] = late_steps[0][:, c0 // PIECE - 2]
+            centre[c0] = both_centres[:, c0 // PIECE - 2]
         for t in range(PACK):
-            nc.scalar.activation(late_steps[0][:, :, t, :], plus[t][:, second_half].rearrange("p (k c) -> p k c", k=2), COPY, scale=2.0)
+            nc.scalar.activation(both_centres[:, :, t, :], plus[t][:, second_half].rearrange("p (k c) -> p k c", k=2), COPY, scale=2.0)
 
         for t in range(PACK):
             east_diff(t, HALF, HALF)
@@ -321,6 +327,7 @@ def tile_picked_minmod_none_po_kernel(
             west_diff(t, HALF, HALF)
         west_diff(PACK - 1, piece2, PIECE)
         west_diff(PACK - 1, piece3, PIECE)
+        held[0] = sb("held", [P, 2, PACK, PIECE], F32, tag="plus0_then_late_steps")
         cap(piece2)
         quantise_early_z()
         second_layer(piece0)

@@ -195,9 +195,7 @@ def tile_picked_minmod_none_po_kernel(
         held = {}
 
         def cap(c0):
-            if c0 < HALF:
-                capped[c0] = shared[:, PACK * (1 + c0 // PIECE) : PACK * (2 + c0 // PIECE), :]
-            elif c0 == HALF:
+            if c0 <= HALF:
                 capped[c0] = sb("u%d" % c0, [P, PACK, PIECE], F32)[:]
             else:
                 capped[c0] = held[0][:, 1]
@@ -233,8 +231,8 @@ def tile_picked_minmod_none_po_kernel(
                     add_transposed(total[c0][:, t, :], below[:, t - planes.start, in_half(c0, PIECE)], False, t == PACK - 1)
 
         def lift(c0):
-            lifted[c0] = sb("lifted%d" % c0, [P, PACK, P], F32)
-            nc.scalar.activation(lifted[c0][:], total[c0][:], RELU, scale=-1.0)
+            lifted[c0] = shared[:, PACK * (1 + c0 // PIECE) : PACK * (2 + c0 // PIECE), :]
+            nc.scalar.activation(lifted[c0], total[c0][:], RELU, scale=-1.0)
 
         def edge_without_limit(c0, number):
             for t in range(PACK):
@@ -304,8 +302,10 @@ def tile_picked_minmod_none_po_kernel(
             east_diff(t, 0, HALF)
             turn_b(t)
             west_diff(t, 0, HALF)
+            if t == 2:
+                turn_below(slice(0, 2))
             if t >= 2:
-                turn_below(slice(0, 3) if t == 2 else slice(3, 4))
+                turn_below(slice(t, t + 1))
         w2_scales_dealt = sb("w2_scales", [P, PACK * P], U8)
         w2_dealt = [(plane(w2_words_dealt, t), plane(w2_scales_dealt, t)) for t in range(PACK)]
         lift(piece0)

from contextlib import ExitStack

import concourse.mybir as mybir
from concourse.masks import make_identity

K, T, S, N, H = 512, 2048, 512, 512, 512
FLOPS = 2 * K * H * S + 2 * H * N * S

F32 = mybir.dt.float32
BF16 = mybir.dt.bfloat16
I32 = mybir.dt.int32
U32 = mybir.dt.uint32
U16 = mybir.dt.uint16
U8 = mybir.dt.uint8
FP8X4 = mybir.dt.float8_e4m3fn_x4
ALU = mybir.AluOpType
COPY = mybir.ActivationFunctionType.Copy
RELU = mybir.ActivationFunctionType.Relu

P = 128
PACK = 4
QUADRANTS = 4
GROUP = 16
HALF = S // 2
PIECE = 128
LINE_BYTES = 16
X_AHEAD = 3 * T // 8
B_SHIFT = HALF + PIECE


def tile_picked_minmod_none_po_kernel(
    tc, x_words, x_scales, w1_words, w1_scales, gn, w2_words, w2_scales, offs, east, west, out_0, out_1, out_2
):
    nc = tc.nc
    with ExitStack() as ctx:
        keep = ctx.enter_context(tc.tile_pool(name="keep", bufs=1))
        psum = ctx.enter_context(tc.psum_pool(name="psum", bufs=1))

        def sb(name, shape, dtype, tag=""):
            return keep.tile(shape, dtype, name=name, tag=tag, align_bytes=64)

        def bank(name, shape, number):
            return psum.tile(shape, F32, name=name, tag="bank%d" % number)

        def words_of(dram):
            return dram[0].rearrange("p n t -> p (n t)").bitcast(I32)

        def load_scale_rows(tile, dram):
            for r in range(4):
                nc.sync.dma_start(out=tile[r:P:32, :].bitcast(I32), in_=dram[0, r:16:4, :].bitcast(I32))

        def entries(list_tile, c0, n):
            return list_tile[:, c0 // GROUP : (c0 + n) // GROUP]

        offs_sb = keep.tile([P, S // GROUP], U16, name="offs_sb")
        east_sb = keep.tile([P, S // GROUP], U16, name="east_sb")
        west_sb = keep.tile([P, S // GROUP], U16, name="west_sb")
        xw = sb("xw", [P, T], U32)
        xs = sb("xs", [P, T], U8)
        w1w = sb("w1w", [P, H], I32)
        w2w = sb("w2w", [P, N], I32)
        w2s = sb("w2s", [P, N], U8)
        gain = sb("gain", [P, PACK], F32)
        w1s = sb("w1s", [P, H], U8, tag="w1s_then_w1_words")

        for scale_tile in (xs, w1s, w2s):
            nc.vector.memset(scale_tile[:].bitcast(I32), 0)

        nc.sync.dma_start(offs_sb[:], offs)
        nc.sync.dma_start(out=xw[:, :X_AHEAD].bitcast(I32), in_=words_of(x_words)[:, :X_AHEAD])
        load_scale_rows(xs, x_scales)
        nc.sync.dma_start(out=xw[:, X_AHEAD:].bitcast(I32), in_=words_of(x_words)[:, X_AHEAD:])
        nc.sync.dma_start(out=w1w[:], in_=words_of(w1_words))
        load_scale_rows(w1s, w1_scales)
        nc.sync.dma_start(out=gain[:], in_=gn.rearrange("(p t) o -> p (t o)", t=PACK))
        nc.sync.dma_start(out=w2w[:], in_=words_of(w2_words))
        nc.sync.dma_start(east_sb[:], east)
        nc.sync.dma_start(west_sb[:], west)
        load_scale_rows(w2s, w2_scales)

        half_gain = sb("half_gain", [P, PACK], F32)
        b_rows = sb("b_rows", [P, B_SHIFT + PACK * HALF], F32)
        minus_half_gain = b_rows[:, :PACK]
        nc.scalar.activation(half_gain[:], gain[:], COPY, scale=0.5)
        nc.scalar.activation(minus_half_gain, gain[:], COPY, scale=-0.5)

        first_plane, other_planes, all_planes = slice(0, 1), slice(1, PACK), slice(0, PACK)
        words_a_line, scales_a_line = LINE_BYTES // 4, LINE_BYTES

        def deal(dealt, source, run, planes):
            nc.vector.tensor_copy(
                out=dealt.rearrange("p (t b i) -> p b t i", t=planes.stop - planes.start, i=run),
                in_=source[:].rearrange("p (b i t) -> p b t i", t=PACK, i=run)[:, :, planes, :],
            )

        w1_first_words = sb("w1_first_words", [P, P], I32)
        w1_scales_dealt = sb("w1_scales", [P, PACK * P], U8)
        identity = sb("identity", [P, P], F32)
        make_identity(nc, identity[:])

        picked_scales = sb("picked_scales", [P, S], U8)
        picked_words = sb("picked_words", [P, S], U32)
        first_half, second_half, all_columns = slice(0, HALF), slice(HALF, S), slice(0, S)
        nc.vector.tensor_copy(picked_scales[:], xs[:].indirect(offs_sb[:]))
        nc.vector.tensor_copy(picked_words[:], xw[:].indirect(offs_sb[:]))
        deal(w1_scales_dealt[:, :P], w1s, scales_a_line, first_plane)
        deal(w1_first_words[:], w1w, words_a_line, first_plane)
        deal(w1_scales_dealt[:, P:], w1s, scales_a_line, other_planes)
        w1_other_words = sb("w1_other_words", [P, (PACK - 1) * P], I32, tag="w1s_then_w1_words")
        deal(w1_other_words[:], w1w, words_a_line, other_planes)

        def plane(tile, t):
            return tile[:, P * t : P * (t + 1)]

        w1_dealt = [(plane(w1_other_words, t - 1) if t else w1_first_words[:], plane(w1_scales_dealt, t)) for t in range(PACK)]

        def product(dst, weights, t, words, scales):
            nc.tensor.matmul_mx(
                out=dst,
                lhsT=weights[t][0].bitcast(FP8X4),
                lhsT_scale=weights[t][1],
                rhs=words.bitcast(FP8X4),
                rhs_scale=scales,
                start=True,
                stop=True,
            )

        plus = [sb("plus%d" % t, [P, S], F32, tag="" if t else "plus0_then_late_steps") for t in range(PACK)]
        minus = [sb("minus%d" % t, [P, S], F32) for t in range(PACK)]

        def first_layer(t, cols, plus_on_vector, number):
            y = bank("y", [P, cols.stop - cols.start], number)
            product(y[:], w1_dealt, t, picked_words[:, cols], picked_scales[:, cols])
            if plus_on_vector:
                nc.vector.tensor_scalar(plus[t][:, cols], y[:], half_gain[:, t : t + 1], None, ALU.mult)
            else:
                nc.scalar.activation(plus[t][:, cols], y[:], COPY, scale=half_gain[:, t : t + 1])
            if t == PACK - 1:
                for half in (first_half, second_half):
                    nc.scalar.activation(minus[t][:, half], y[:, half], COPY, scale=minus_half_gain[:, t : t + 1])
            else:
                nc.scalar.activation(minus[t][:, cols], y[:], COPY, scale=minus_half_gain[:, t : t + 1])

        first_layer(0, first_half, False, 0)
        first_layer(0, second_half, False, 1)
        for t in range(1, PACK):
            first_layer(t, all_columns, False, t + 1)

        w2_words_dealt = sb("w2_words", [P, PACK * P], I32)
        deal(w2_words_dealt[:], w2w, words_a_line, all_planes)

        def add_transposed(dst, src, start, stop):
            nc.tensor.matmul(dst, src, identity[:], is_transpose=True, start=start, stop=stop)

        turned = {}
        for c0 in range(0, HALF, PIECE):
            turned[c0] = bank("turned", [P, PACK, P], 5 + c0 // PIECE)
            for t in range(PACK):
                add_transposed(turned[c0][:, t, :], plus[t][:, c0 : c0 + PIECE], t == 0, False)
                add_transposed(turned[c0][:, t, :], plus[t][:, c0 : c0 + PIECE], False, False)

        a_tiles = {}

        def b_planes(c0):
            start = B_SHIFT if c0 < HALF else 0
            return b_rows[:, start : start + PACK * HALF].rearrange("p (t c) -> p t c", t=PACK)

        def a_planes(c0):
            h0 = c0 - c0 % HALF
            if h0 not in a_tiles:
                a_tiles[h0] = sb("a%d" % h0, [P, PACK, HALF], F32, tag="a")
            return a_tiles[h0]

        def in_a(c0, n):
            return in_half(c0, n)

        def in_half(c0, n):
            return slice(c0 % HALF, c0 % HALF + n)

        def east_diff(t, c0, n):
            nc.vector.tensor_tensor(
                b_planes(c0)[:, t, in_half(c0, n)], plus[t][:].indirect(entries(east_sb, c0, n)), minus[t][:, c0 : c0 + n], ALU.add
            )

        def west_diff(t, c0, n):
            nc.vector.tensor_tensor(
                a_planes(c0)[:, t, in_a(c0, n)], minus[t][:].indirect(entries(west_sb, c0, n)), plus[t][:, c0 : c0 + n], ALU.add
            )

        capped, limited, z_bf16, z_mx, out_bf16, out_f32 = {}, {}, {}, {}, {}, {}

        z_early = sb("z_early", [P, HALF * PACK], BF16)
        centre = {}
        shared = sb("shared", [P, 3 * PACK, PIECE], F32)
        held = {}

        def cap(c0):
            if c0 <= HALF:
                capped[c0] = sb("u%d" % c0, [P, PACK, PIECE], F32)[:]
            else:
                capped[c0] = held[0][:, 1]
            cols = in_half(c0, PIECE)
            nc.vector.scalar_tensor_tensor(capped[c0], a_planes(c0)[:, :, in_a(c0, PIECE)], 0.0, b_planes(c0)[:, :, cols], ALU.max, ALU.min)

        def limit(c0):
            limited[c0] = held[0][:, 0] if c0 == HALF else sb("m%d" % c0, [P, PACK, PIECE], F32)[:]
            nc.vector.scalar_tensor_tensor(limited[c0], a_planes(c0)[:, :, in_a(c0, PIECE)], 0.0, capped[c0], ALU.min, ALU.max)

        def edge_on_vector(c0):
            z_bf16[c0] = sb("z%d" % c0, [P, PIECE * PACK], BF16)
            nc.vector.tensor_tensor(
                z_bf16[c0][:].rearrange("p (c i t) -> p c t i", t=PACK, i=2),
                limited[c0].rearrange("p t (c i) -> p c t i", i=2),
                centre[c0].rearrange("p t (c i) -> p c t i", i=2),
                ALU.add,
            )

        lifted = {}

        total = {0: bank("total", [P, PACK, P], 7), PIECE: bank("total", [P, PACK, P], 0)}

        def turn_b(t):
            for c0 in total:
                add_transposed(total[c0][:, t, :], b_planes(c0)[:, t, in_half(c0, PIECE)], t == 0, False)

        def turn_below(planes):
            below = sb("below", [P, planes.stop - planes.start, HALF], F32, tag="below%d_then_w2" % planes.start)
            nc.scalar.activation(below[:], a_planes(0)[:, planes, :], RELU, scale=-1.0)
            for c0 in total:
                for t in range(planes.start, planes.stop):
                    add_transposed(total[c0][:, t, :], below[:, t - planes.start, in_half(c0, PIECE)], False, t == PACK - 1)

        def lift(c0):
            lifted[c0] = shared[:, PACK * (1 + c0 // PIECE) : PACK * (2 + c0 // PIECE), :]
            nc.scalar.activation(lifted[c0], total[c0][:], RELU, scale=-1.0)

        def edge_without_limit(c0, number):
            for t in range(PACK):
                add_transposed(turned[c0][:, t, :], capped[c0][:, t, :], False, t == PACK - 1)
            summed = shared[:, :PACK, :] if c0 else sb("summed0", [P, PACK, P], F32)[:]
            nc.scalar.copy(summed, turned[c0][:])
            whole = bank("whole", [P, PACK, P], number)
            for t in range(PACK):
                add_transposed(whole[:, t, :], lifted[c0][:, t, :], t == 0, False)
            for t in range(PACK):
                add_transposed(whole[:, t, :], summed[:, t, :], False, t == PACK - 1)
            nc.scalar.copy(z_early[:, c0 * PACK : (c0 + PIECE) * PACK].rearrange("p (j t) -> p j t", t=PACK), whole[:].rearrange("p t j -> p j t"))

        def quantise_z(c0):
            z_mx[c0] = (sb("zw%d" % c0, [P, PIECE], U32), sb("zs%d" % c0, [P, PIECE], U8))
            nc.vector.quantize_mx(out=z_mx[c0][0][:].bitcast(FP8X4), scales=z_mx[c0][1][:], in_=z_bf16[c0][:])

        def quantise_early_z():
            words, scales = sb("zw_early", [P, HALF], U32), sb("zs_early", [P, HALF], U8)
            nc.vector.quantize_mx(out=words[:].bitcast(FP8X4), scales=scales[:], in_=z_early[:])
            for c0 in range(0, HALF, PIECE):
                z_mx[c0] = (words[:, c0 : c0 + PIECE], scales[:, c0 : c0 + PIECE])

        out_rows = out_0.rearrange("(p t) j -> p t j", t=PACK)
        out_words = out_1[0].rearrange("p n t -> p (n t)").bitcast(I32)
        out_scales = sb("out_scales", [P, S], U8)

        def second_layer(c0):
            zw, zs = z_mx[c0]
            result = sb("result%d" % c0, [P, PACK, PIECE], F32)
            rounded = sb("rounded%d" % c0, [P, PIECE, PACK], BF16)
            if c0 >= HALF:
                for pair in range(0, PACK, 2):
                    acc = bank("acc", [P, 2, PIECE], (2 * (c0 // PIECE) + pair // 2 + 1) % 8)
                    for t in range(2):
                        product(acc[:, t, :], w2_dealt, pair + t, zw[:], zs[:])
                    nc.scalar.copy(result[:, pair : pair + 2, :], acc[:])
            else:
                acc = bank("acc", [P, PACK, PIECE], 3 + c0 // PIECE)
                for t in range(PACK):
                    product(acc[:, t, :], w2_dealt, t, zw[:], zs[:])
                nc.scalar.copy(rounded[:], acc[:].rearrange("p t n -> p n t"))
                nc.scalar.copy(result[:], acc[:])
            nc.sync.dma_start(out=out_rows[:, :, c0 : c0 + PIECE], in_=result[:])
            out_bf16[c0] = rounded
            out_f32[c0] = result

        def round_on_vector(c0):
            nc.vector.tensor_copy(
                out_bf16[c0][:].rearrange("p (c i) t -> p c t i", i=4), out_f32[c0][:].rearrange("p t (c i) -> p c t i", i=4)
            )

        out_codes = sb("out_codes", [P, S], U32)

        def quantise_out(c0):
            nc.vector.quantize_mx(
                out=out_codes[:, c0 : c0 + PIECE].bitcast(FP8X4),
                scales=out_scales[:, c0 : c0 + PIECE],
                in_=out_bf16[c0][:].rearrange("p n t -> p (n t)"),
            )

        def store_codes(cols):
            nc.sync.dma_start(out=out_words[:, cols], in_=out_codes[:, cols].bitcast(I32))

        piece0, piece1, piece2, piece3 = range(0, S, PIECE)
        for t in range(PACK):
            east_diff(t, 0, HALF)
            turn_b(t)
            west_diff(t, 0, HALF)
            if t == 2:
                turn_below(slice(0, 2))
            if t >= 2:
                turn_below(slice(t, t + 1))
        w2_scales_dealt = sb("w2_scales", [P, PACK * P], U8)
        w2_dealt = [(plane(w2_words_dealt, t), plane(w2_scales_dealt, t)) for t in range(PACK)]
        lift(piece0)
        lift(piece1)
        cap(piece0)
        cap(piece1)
        deal(w2_scales_dealt[:], w2s, scales_a_line, all_planes)
        edge_without_limit(piece0, 1)
        edge_without_limit(piece1, 2)
        both_centres = shared[:, 2 : 2 + 2 * PACK, :].rearrange("p (t k) c -> p k t c", k=2)
        for c0 in (piece2, piece3):
            centre[c0] = both_centres[:, c0 // PIECE - 2]
        for t in range(PACK):
            nc.scalar.activation(both_centres[:, :, t, :], plus[t][:, second_half].rearrange("p (k c) -> p k c", k=2), COPY, scale=2.0)

        for t in range(PACK):
            east_diff(t, HALF, HALF)
        for t in range(PACK - 1):
            west_diff(t, HALF, HALF)
        west_diff(PACK - 1, piece2, PIECE)
        west_diff(PACK - 1, piece3, PIECE)
        held[0] = sb("held", [P, 2, PACK, PIECE], F32, tag="plus0_then_late_steps")
        cap(piece2)
        quantise_early_z()
        second_layer(piece0)
        second_layer(piece1)
        limit(piece2)
        cap(piece3)
        edge_on_vector(piece2)
        limit(piece3)
        quantise_z(piece2)
        second_layer(piece2)
        edge_on_vector(piece3)
        quantise_out(piece0)
        quantise_z(piece3)
        second_layer(piece3)
        quantise_out(piece1)
        round_on_vector(piece2)
        quantise_out(piece2)
        store_codes(slice(0, piece3))
        round_on_vector(piece3)
        quantise_out(piece3)
        store_codes(slice(piece3, S))
        for q in range(QUADRANTS):
            (nc.sync if q % 2 else nc.scalar).dma_start(
                out=out_2[0, 4 * q : 4 * q + 4, :].bitcast(I32), in_=out_scales[32 * q : 32 * q + 4, :].bitcast(I32)
            )
